import numpy as np
import ml_dtypes


def mxq(x, axis, fmt="e4m3"):
    dtype, down = {"e4m3": (ml_dtypes.float8_e4m3fn, 7), "e5m2": (ml_dtypes.float8_e5m2, 14)}[fmt]
    v = np.moveaxis(np.asarray(x, np.float32).astype(ml_dtypes.bfloat16).astype(np.float64), axis, -1)
    blocks = v.reshape(v.shape[:-1] + (-1, 32))
    amax = np.abs(blocks).max(-1, keepdims=True)
    byte = np.maximum(np.where(amax > 0, np.frexp(amax)[1] - 1 + 127, 0) - down, 1)
    scale = np.exp2(byte - 127.0)
    codes = (blocks / scale).astype(np.float32).astype(dtype).astype(np.float64)
    return np.moveaxis((codes * scale).reshape(v.shape), -1, axis)


WIDE = False


def mx_kscale(k):
    if not WIDE:
        return np.ones(k)
    levels = np.array([10, -10, 5, -5, 0])
    if k % 512:
        return np.exp2(np.random.permutation(np.resize(levels, k // 32))).repeat(32)
    a = np.empty((k // 512, 16))
    for p in range(k // 512):
        a[p, :8] = np.random.permutation(np.resize(levels, 8))
        for g in range(8):
            far = levels[np.abs(levels - a[p, g]) >= 10]
            a[p, g + 8] = far[np.random.randint(len(far))]
    return np.exp2(a.ravel()).repeat(32)


def f64(x):
    return np.asarray(x).astype(np.float64)


def striped(idx):
    return np.tile(idx.reshape(-1, 16).T, (8, 1)).astype(np.uint16)


def unstriped(offs):
    return offs[:16].T.reshape(-1).astype(np.int64)


def pack_weight(w):
    k, n = w.shape
    w = f64(np.asarray(w, np.float32).astype(ml_dtypes.bfloat16)).reshape(k // 32, 32, n)
    amax = np.abs(w).max(1)
    byte = np.clip(np.where(amax > 0, np.frexp(amax)[1] - 1 + 127 - 7, 1), 1, 254)
    scaled = (w * np.exp2(127.0 - byte)[:, None, :]).reshape(k, n).astype(np.float32)
    words = np.ascontiguousarray(scaled.reshape(k // 512, 128, 4, n).transpose(0, 1, 3, 2)).astype(ml_dtypes.float8_e4m3fn).view(np.uint8)
    return words, np.ascontiguousarray(byte.astype(np.uint8).reshape(k // 512, 16, n))


def unpack_weight(words, scales):
    g, p, n, _ = words.shape
    vals = np.ascontiguousarray(words).view(ml_dtypes.float8_e4m3fn).astype(np.float64) * np.repeat(np.exp2(scales.astype(np.float64) - 127.0), 8, axis=1)[..., None]
    return vals.transpose(0, 1, 3, 2).reshape(g * 512, n)


def silu(v):
    return v / (1.0 + np.exp(-np.maximum(v, -700.0)))


K, T, S, D, V, H, N = 512, 1024, 512, 2, 256, 512, 256
P = 2 ** 7


def setup_inputs():
    n = np.random.standard_normal
    s = mx_kscale(K)[:, None]
    u = mx_kscale(H)
    packed_w2 = pack_weight(n((H, N)) / np.sqrt(H) / u[:, None])
    return {
        "xT": (n((K, T)) * s).astype(np.float32),
        "w1": (n((K, H)) / np.sqrt(K) / s * u).astype(np.float32),
        "w2_words": packed_w2[0],
        "w2_scales": packed_w2[1],
        "gate": (np.tile(np.random.uniform(0.2, 1.0, (D, 1, V)) / np.sqrt(D), (1, P, 1))).astype(np.float32),
        "offs": striped(np.random.permutation(T)[:S]),
        "cen": striped(np.random.permutation(S)[:V]),
        "pos1": striped(np.random.permutation(S)[:V]),
        "pos2": striped(np.random.permutation(S)[:V]),
    }


def reference(xT, w1, w2_words, w2_scales, gate, offs, cen, pos1, pos2):
    xq = mxq(f64(xT)[:, unstriped(offs)], 0, "e4m3")
    h = silu(mxq(f64(w1), 0, "e4m3").T @ xq)
    z = h[:, unstriped(cen)] - (h[:, unstriped(pos1)] * f64(gate)[0, :1] + h[:, unstriped(pos2)] * f64(gate)[1, :1])
    return unpack_weight(w2_words, w2_scales).T @ mxq(z, 0, "e4m3")

@@ -1,0 +1,183 @@
+from contextlib import ExitStack
+
+import concourse.mybir as mybir
+
+K, T, S, D, V, H, N = 512, 1024, 512, 2, 256, 512, 256
+FLOPS = 2 * K * H * S + 2 * H * N * V
+
+F32 = mybir.dt.float32
+BF16 = mybir.dt.bfloat16
+I32 = mybir.dt.int32
+U32 = mybir.dt.uint32
+U16 = mybir.dt.uint16
+U8 = mybir.dt.uint8
+FP8X4 = mybir.dt.float8_e4m3fn_x4
+MULT = mybir.AluOpType.mult
+SUB = mybir.AluOpType.subtract
+SILU = mybir.ActivationFunctionType.Silu
+
+P = 128
+PACK = 4
+STRIPE = 16
+
+
+def tile_picked_lapl_silu_e_kernel(
+    tc, xT, w1, w2_words, w2_scales, gate, offs, cen, pos1, pos2, out
+):
+    nc = tc.nc
+    SH = S // 2
+    VH = V // 2
+    MH = P // 2
+
+    with ExitStack() as ctx:
+        keep = ctx.enter_context(tc.tile_pool(name="keep", bufs=1))
+        psum = ctx.enter_context(tc.psum_pool(name="psum", bufs=8))
+
+        def bank(name):
+            return psum.tile([P, 512], F32, name=name, tag="bank")
+
+        x_rows = xT.rearrange("(p j) t -> p j t", j=PACK)
+        w_rows = w1.rearrange("(p j) c -> p j c", j=PACK)
+        x_plane = [keep.tile([P, T], F32, name=f"x_plane{j}") for j in range(PACK)]
+        offs_sb = keep.tile([P, S // STRIPE], U16)
+        nc.sync.dma_start(x_plane[0][:], x_rows[:, 0, :])
+        nc.sync.dma_start(offs_sb[:], offs)
+        for j in range(1, PACK):
+            nc.sync.dma_start(x_plane[j][:], x_rows[:, j, :])
+        w_half = [keep.tile([P, PACK, H // 2], F32, name=f"w_half{c}") for c in range(2)]
+        for c in range(2):
+            nc.sync.dma_start(w_half[c][:], w_rows[:, :, c * (H // 2) : (c + 1) * (H // 2)])
+        gate_sb = keep.tile([P, D, V], F32)
+        nc.sync.dma_start(gate_sb[:], gate.rearrange("d p v -> p d v"))
+        pos1_sb = keep.tile([P, V // STRIPE], U16)
+        pos2_sb = keep.tile([P, V // STRIPE], U16)
+        cen_sb = keep.tile([P, V // STRIPE], U16)
+        nc.sync.dma_start(pos1_sb[:], pos1)
+        nc.sync.dma_start(pos2_sb[:], pos2)
+        nc.sync.dma_start(cen_sb[:], cen)
+        w2_codes = keep.tile([P, N], I32, align_bytes=64)
+        nc.sync.dma_start(w2_codes[:], w2_words[0].rearrange("p n t -> p (n t)").bitcast(I32))
+        w2_plane = keep.tile([P, N], U8, align_bytes=64)
+        nc.gpsimd.memset(w2_plane[:], 0)
+        for q in range(4):
+            nc.sync.dma_start(
+                w2_plane[32 * q : 32 * q + 4, :].bitcast(I32), w2_scales[0, 4 * q : 4 * q + 4, :].bitcast(I32)
+            )
+
+        picked = [keep.tile([P, PACK, SH], BF16, name=f"picked{s}") for s in range(2)]
+        cols = SH // STRIPE
+        for j in range(PACK):
+            for s in range(2):
+                nc.vector.tensor_copy(picked[s][:, j, :], x_plane[j][:].indirect(offs_sb[:, s * cols : (s + 1) * cols]))
+
+        x_grouped = [keep.tile([P, SH, PACK], BF16, name=f"x_grouped{s}", align_bytes=64) for s in range(2)]
+
+        def weave(copy, s, lo, hi):
+            copy(
+                x_grouped[s][:, lo:hi, :].rearrange("p (c i) j -> p c j i", i=4),
+                picked[s][:, :, lo:hi].rearrange("p j (c i) -> p c j i", i=4),
+            )
+
+        w_pair = [keep.tile([P, 2, P, PACK], BF16, name=f"w_pair{u}", align_bytes=64) for u in range(2)]
+
+        def deal(u, c):
+            nc.scalar.copy(
+                w_pair[u][:, :, c * MH : (c + 1) * MH, :].rearrange("p e m j -> p m j e"),
+                w_half[c][:].rearrange("p j (m t) -> p m j t", t=PACK)[:, :, :, 2 * u : 2 * u + 2],
+            )
+
+        weave(nc.scalar.copy, 0, 0, SH // 2)
+        weave(nc.vector.tensor_copy, 0, SH // 2, SH)
+        weave(nc.vector.tensor_copy, 1, 0, SH)
+        deal(0, 0)
+        deal(0, 1)
+
+        x_codes = keep.tile([P, S], U32, align_bytes=64)
+        x_scales = keep.tile([P, S], U8, align_bytes=64)
+        for s in range(2):
+            nc.vector.quantize_mx(
+                x_codes[:, s * SH : (s + 1) * SH].bitcast(FP8X4),
+                x_scales[:, s * SH : (s + 1) * SH],
+                x_grouped[s][:].rearrange("p n j -> p (n j)"),
+            )
+
+        w_codes = [keep.tile([P, P], U32, name=f"w_codes{t}", align_bytes=64) for t in range(PACK)]
+        w_scales = [keep.tile([P, P], U8, name=f"w_scales{t}", align_bytes=64) for t in range(PACK)]
+        h = [keep.tile([P, S], F32, name=f"h{t}") for t in range(PACK)]
+
+        def quantise_w(t):
+            nc.vector.quantize_mx(
+                w_codes[t][:].bitcast(FP8X4),
+                w_scales[t][:],
+                w_pair[t // 2][:, t % 2, :, :].rearrange("p m j -> p (m j)"),
+            )
+
+        def project(t, lo, hi):
+            acc = bank(f"pre{t}_{lo}")
+            nc.tensor.matmul_mx(
+                acc[:, : hi - lo],
+                lhsT=w_codes[t][:].bitcast(FP8X4),
+                lhsT_scale=w_scales[t][:],
+                rhs=x_codes[:, lo:hi].bitcast(FP8X4),
+                rhs_scale=x_scales[:, lo:hi],
+                start=True,
+                stop=True,
+            )
+            nc.scalar.activation(h[t][:, lo:hi], acc[:, : hi - lo], SILU)
+
+        quantise_w(0)
+        quantise_w(1)
+        project(0, 0, SH)
+        project(0, SH, S)
+        project(1, 0, S)
+        deal(1, 0)
+        deal(1, 1)
+
+        less_first = keep.tile([P, PACK, V], F32)
+        second = keep.tile([P, PACK, V], F32)
+
+        def neighbours(t):
+            first = keep.tile([P, V], F32, name=f"first{t}")
+            nc.vector.tensor_tensor(first[:], h[t][:].indirect(pos1_sb[:]), gate_sb[:, 0, :], MULT)
+            nc.vector.tensor_tensor(second[:, t, :], h[t][:].indirect(pos2_sb[:]), gate_sb[:, 1, :], MULT)
+            nc.vector.tensor_tensor(less_first[:, t, :], h[t][:].indirect(cen_sb[:]), first[:], SUB)
+
+        neighbours(0)
+        for t in (2, 3):
+            quantise_w(t)
+            project(t, 0, S)
+        for t in range(1, PACK):
+            neighbours(t)
+
+        z_grouped = [keep.tile([P, VH, PACK], BF16, name=f"z_grouped{b}", align_bytes=64) for b in range(2)]
+        z_codes = [keep.tile([P, VH], U32, name=f"z_codes{b}", align_bytes=64) for b in range(2)]
+        z_scales = [keep.tile([P, VH], U8, name=f"z_scales{b}", align_bytes=64) for b in range(2)]
+        for b in range(2):
+            vs = slice(b * VH, (b + 1) * VH)
+            nc.vector.tensor_tensor(
+                z_grouped[b][:].rearrange("p (c i) t -> p c t i", i=2),
+                less_first[:, :, vs].rearrange("p t (c i) -> p c t i", i=2),
+                second[:, :, vs].rearrange("p t (c i) -> p c t i", i=2),
+                SUB,
+            )
+        for b in range(2):
+            nc.vector.quantize_mx(
+                z_codes[b][:].bitcast(FP8X4), z_scales[b][:], z_grouped[b][:].rearrange("p v t -> p (v t)")
+            )
+        out_rows = out.rearrange("(g p) v -> p g v", p=P)
+        for b in range(2):
+            result = keep.tile([P, 2, VH], F32, name=f"result{b}")
+            for g, copy in enumerate((nc.scalar.copy, nc.vector.tensor_copy)):
+                acc = bank(f"acc{b}_{g}")
+                ms = slice(g * P, (g + 1) * P)
+                nc.tensor.matmul_mx(
+                    acc[:, :VH],
+                    lhsT=w2_codes[:, ms].bitcast(FP8X4),
+                    lhsT_scale=w2_plane[:, ms],
+                    rhs=z_codes[b][:].bitcast(FP8X4),
+                    rhs_scale=z_scales[b][:],
+                    start=True,
+                    stop=True,
+                )
+                copy(result[:, g, :], acc[:, :VH])
+            nc.sync.dma_start(out_rows[:, :, b * VH : (b + 1) * VH], result[:])

@@ -36,14 +36,20 @@ def tile_picked_lapl_silu_e_kernel(
         def bank(name):
             return psum.tile([P, 512], F32, name=name, tag="bank")
 
+        warm = keep.tile([P, 8], F32)
+        nc.vector.memset(warm[:], 0.0)
+        warm_out = keep.tile([P, 8], F32)
+        nc.scalar.activation(warm_out[:], warm[:], SILU)
         x_rows = xT.rearrange("(p j) t -> p j t", j=PACK)
         w_rows = w1.rearrange("(p j) c -> p j c", j=PACK)
-        x_plane = [keep.tile([P, T], F32, name=f"x_plane{j}") for j in range(PACK)]
+        chunks = ((0, 0, 512), (0, 512, 1024), (1, 0, 512), (1, 512, 768), (1, 768, 1024))
+        x_chunk = {}
         offs_sb = keep.tile([P, S // STRIPE], U16)
-        nc.sync.dma_start(x_plane[0][:], x_rows[:, 0, :])
-        nc.sync.dma_start(offs_sb[:], offs)
-        for j in range(1, PACK):
-            nc.sync.dma_start(x_plane[j][:], x_rows[:, j, :])
+        for u, lo, hi in chunks:
+            x_chunk[u, lo] = keep.tile([P, 2, hi - lo], F32, name=f"x_chunk{u}_{lo}")
+            nc.sync.dma_start(x_chunk[u, lo][:], x_rows[:, 2 * u : 2 * u + 2, lo:hi])
+            if (u, lo) == (0, 0):
+                nc.sync.dma_start(offs_sb[:], offs)
         w_half = [keep.tile([P, PACK, H // 2], F32, name=f"w_half{c}") for c in range(2)]
         for c in range(2):
             nc.sync.dma_start(w_half[c][:], w_rows[:, :, c * (H // 2) : (c + 1) * (H // 2)])
@@ -64,19 +70,28 @@ def tile_picked_lapl_silu_e_kernel(
                 w2_plane[32 * q : 32 * q + 4, :].bitcast(I32), w2_scales[0, 4 * q : 4 * q + 4, :].bitcast(I32)
             )
 
-        picked = [keep.tile([P, PACK, SH], BF16, name=f"picked{s}") for s in range(2)]
-        cols = SH // STRIPE
-        for j in range(PACK):
-            for s in range(2):
-                nc.vector.tensor_copy(picked[s][:, j, :], x_plane[j][:].indirect(offs_sb[:, s * cols : (s + 1) * cols]))
-
+        pairs = [keep.tile([P, T, 2], BF16, name=f"pairs{u}") for u in range(2)]
         x_grouped = [keep.tile([P, SH, PACK], BF16, name=f"x_grouped{s}", align_bytes=64) for s in range(2)]
+        cols = SH // STRIPE
 
-        def weave(copy, s, lo, hi):
+        def pair_up(copy, u, lo, a, b):
             copy(
-                x_grouped[s][:, lo:hi, :].rearrange("p (c i) j -> p c j i", i=4),
-                picked[s][:, :, lo:hi].rearrange("p j (c i) -> p c j i", i=4),
+                pairs[u][:, lo + a : lo + b, :].rearrange("p (c i) e -> p c e i", i=4),
+                x_chunk[u, lo][:, :, a:b].rearrange("p e (c i) -> p c e i", i=4),
             )
+
+        for u in range(2):
+            mine = [(lo, hi) for uu, lo, hi in chunks if uu == u]
+            for lo, hi in mine[:-1]:
+                pair_up(nc.scalar.copy, u, lo, 0, hi - lo)
+            lo, hi = mine[-1]
+            cut = (hi - lo) * 3 // 8
+            pair_up(nc.scalar.copy, u, lo, 0, cut)
+            pair_up(nc.vector.tensor_copy, u, lo, cut, hi - lo)
+            window = pairs[u][:].rearrange("p n e -> p (n e)").bitcast(U32)
+            for s in range(2):
+                words = x_grouped[s][:].rearrange("p n j -> p (n j)").bitcast(U32).rearrange("p (n u) -> p n u", u=2)
+                nc.vector.tensor_copy(words[:, :, u], window.indirect(offs_sb[:, s * cols : (s + 1) * cols]))
 
         w_pair = [keep.tile([P, 2, P, PACK], BF16, name=f"w_pair{u}", align_bytes=64) for u in range(2)]
 
@@ -86,9 +101,6 @@ def tile_picked_lapl_silu_e_kernel(
                 w_half[c][:].rearrange("p j (m t) -> p m j t", t=PACK)[:, :, :, 2 * u : 2 * u + 2],
             )
 
-        weave(nc.scalar.copy, 0, 0, SH // 2)
-        weave(nc.vector.tensor_copy, 0, SH // 2, SH)
-        weave(nc.vector.tensor_copy, 1, 0, SH)
         deal(0, 0)
         deal(0, 1)
 
@@ -125,13 +137,14 @@ def tile_picked_lapl_silu_e_kernel(
             )
             nc.scalar.activation(h[t][:, lo:hi], acc[:, : hi - lo], SILU)
 
-        quantise_w(0)
-        quantise_w(1)
-        project(0, 0, SH)
-        project(0, SH, S)
-        project(1, 0, S)
         deal(1, 0)
         deal(1, 1)
+        quantise_w(0)
+        project(0, 0, SH)
+        project(0, SH, S)
+        for t in range(1, PACK):
+            quantise_w(t)
+            project(t, 0, S)
 
         less_first = keep.tile([P, PACK, V], F32)
         second = keep.tile([P, PACK, V], F32)
@@ -142,11 +155,7 @@ def tile_picked_lapl_silu_e_kernel(
             nc.vector.tensor_tensor(second[:, t, :], h[t][:].indirect(pos2_sb[:]), gate_sb[:, 1, :], MULT)
             nc.vector.tensor_tensor(less_first[:, t, :], h[t][:].indirect(cen_sb[:]), first[:], SUB)
 
-        neighbours(0)
-        for t in (2, 3):
-            quantise_w(t)
-            project(t, 0, S)
-        for t in range(1, PACK):
+        for t in range(PACK):
             neighbours(t)
 
         z_grouped = [keep.tile([P, VH, PACK], BF16, name=f"z_grouped{b}", align_bytes=64) for b in range(2)]

@@ -19,40 +19,47 @@ SILU = mybir.ActivationFunctionType.Silu
 P = 128
 PACK = 4
 STRIPE = 16
+BANK = 512
+QUADRANT = 32
+S_HALF = S // 2
+V_HALF = V // 2
+H_HALF = H // 2
+
+LOAD_NODES = (512, 256)
+SCALAR_NODES = 192
+RUN = 4
 
 
 def tile_picked_lapl_silu_e_kernel(
     tc, xT, w1, w2_words, w2_scales, gate, offs, cen, pos1, pos2, out
 ):
     nc = tc.nc
-    SH = S // 2
-    VH = V // 2
-    MH = P // 2
 
     with ExitStack() as ctx:
         keep = ctx.enter_context(tc.tile_pool(name="keep", bufs=1))
         psum = ctx.enter_context(tc.psum_pool(name="psum", bufs=8))
 
         def bank(name):
-            return psum.tile([P, 512], F32, name=name, tag="bank")
+            return psum.tile([P, BANK], F32, name=name, tag="bank")
 
         warm = keep.tile([P, 8], F32)
         nc.vector.memset(warm[:], 0.0)
         warm_out = keep.tile([P, 8], F32)
         nc.scalar.activation(warm_out[:], warm[:], SILU)
+
         x_rows = xT.rearrange("(p j) t -> p j t", j=PACK)
         w_rows = w1.rearrange("(p j) c -> p j c", j=PACK)
-        chunks = ((0, 0, 512), (0, 512, 1024), (1, 0, 512), (1, 512, 768), (1, 768, 1024))
-        x_chunk = {}
+        x_load = {}
         offs_sb = keep.tile([P, S // STRIPE], U16)
-        for u, lo, hi in chunks:
-            x_chunk[u, lo] = keep.tile([P, 2, hi - lo], F32, name=f"x_chunk{u}_{lo}")
-            nc.sync.dma_start(x_chunk[u, lo][:], x_rows[:, 2 * u : 2 * u + 2, lo:hi])
-            if (u, lo) == (0, 0):
-                nc.sync.dma_start(offs_sb[:], offs)
-        w_half = [keep.tile([P, PACK, H // 2], F32, name=f"w_half{c}") for c in range(2)]
+        for u, nodes in enumerate(LOAD_NODES):
+            for lo in range(0, T, nodes):
+                x_load[u, lo] = keep.tile([P, 2, nodes], F32, name=f"x_load{u}_{lo}")
+                nc.sync.dma_start(x_load[u, lo][:], x_rows[:, 2 * u : 2 * u + 2, lo : lo + nodes])
+                if (u, lo) == (0, 0):
+                    nc.sync.dma_start(offs_sb[:], offs)
+        w_half = [keep.tile([P, PACK, H_HALF], F32, name=f"w_half{c}") for c in range(2)]
         for c in range(2):
-            nc.sync.dma_start(w_half[c][:], w_rows[:, :, c * (H // 2) : (c + 1) * (H // 2)])
+            nc.sync.dma_start(w_half[c][:], w_rows[:, :, c * H_HALF : (c + 1) * H_HALF])
         gate_sb = keep.tile([P, D, V], F32)
         nc.sync.dma_start(gate_sb[:], gate.rearrange("d p v -> p d v"))
         pos1_sb = keep.tile([P, V // STRIPE], U16)
@@ -61,43 +68,51 @@ def tile_picked_lapl_silu_e_kernel(
         nc.sync.dma_start(pos1_sb[:], pos1)
         nc.sync.dma_start(pos2_sb[:], pos2)
         nc.sync.dma_start(cen_sb[:], cen)
+
         w2_codes = keep.tile([P, N], I32, align_bytes=64)
         nc.sync.dma_start(w2_codes[:], w2_words[0].rearrange("p n t -> p (n t)").bitcast(I32))
-        w2_plane = keep.tile([P, N], U8, align_bytes=64)
-        nc.gpsimd.memset(w2_plane[:], 0)
-        for q in range(4):
+        w2_scale_sb = keep.tile([P, N], U8, align_bytes=64)
+        nc.gpsimd.memset(w2_scale_sb[:], 0)
+        for q in range(P // QUADRANT):
             nc.sync.dma_start(
-                w2_plane[32 * q : 32 * q + 4, :].bitcast(I32), w2_scales[0, 4 * q : 4 * q + 4, :].bitcast(I32)
+                w2_scale_sb[QUADRANT * q : QUADRANT * q + 4, :].bitcast(I32),
+                w2_scales[0, 4 * q : 4 * q + 4, :].bitcast(I32),
             )
 
         pairs = [keep.tile([P, T, 2], BF16, name=f"pairs{u}") for u in range(2)]
-        x_grouped = [keep.tile([P, SH, PACK], BF16, name=f"x_grouped{s}", align_bytes=64) for s in range(2)]
-        cols = SH // STRIPE
+        x_grouped = [keep.tile([P, S_HALF, PACK], BF16, name=f"x_grouped{s}", align_bytes=64) for s in range(2)]
+        offs_cols = S_HALF // STRIPE
 
-        def pair_up(copy, u, lo, a, b):
+        def pair_up(copy, u, lo, first_node, end_node):
             copy(
-                pairs[u][:, lo + a : lo + b, :].rearrange("p (c i) e -> p c e i", i=4),
-                x_chunk[u, lo][:, :, a:b].rearrange("p e (c i) -> p c e i", i=4),
+                pairs[u][:, lo + first_node : lo + end_node, :].rearrange("p (c i) e -> p c e i", i=RUN),
+                x_load[u, lo][:, :, first_node:end_node].rearrange("p e (c i) -> p c e i", i=RUN),
             )
 
-        for u in range(2):
-            mine = [(lo, hi) for uu, lo, hi in chunks if uu == u]
-            for lo, hi in mine[:-1]:
-                pair_up(nc.scalar.copy, u, lo, 0, hi - lo)
-            lo, hi = mine[-1]
-            cut = (hi - lo) * 3 // 8
-            pair_up(nc.scalar.copy, u, lo, 0, cut)
-            pair_up(nc.vector.tensor_copy, u, lo, cut, hi - lo)
+        def gather_pairs(u):
             window = pairs[u][:].rearrange("p n e -> p (n e)").bitcast(U32)
             for s in range(2):
-                words = x_grouped[s][:].rearrange("p n j -> p (n j)").bitcast(U32).rearrange("p (n u) -> p n u", u=2)
-                nc.vector.tensor_copy(words[:, :, u], window.indirect(offs_sb[:, s * cols : (s + 1) * cols]))
+                grouped = x_grouped[s][:].rearrange("p n j -> p (n j)").bitcast(U32)
+                nc.vector.tensor_copy(
+                    grouped.rearrange("p (n u) -> p n u", u=2)[:, :, u],
+                    window.indirect(offs_sb[:, s * offs_cols : (s + 1) * offs_cols]),
+                )
+
+        first_nodes, second_nodes = LOAD_NODES
+        pair_up(nc.scalar.copy, 0, 0, 0, first_nodes)
+        pair_up(nc.scalar.copy, 0, first_nodes, 0, SCALAR_NODES)
+        pair_up(nc.vector.tensor_copy, 0, first_nodes, SCALAR_NODES, first_nodes)
+        gather_pairs(0)
+        for lo in range(0, T, second_nodes):
+            pair_up(nc.scalar.copy, 1, lo, 0, second_nodes)
+        gather_pairs(1)
 
         w_pair = [keep.tile([P, 2, P, PACK], BF16, name=f"w_pair{u}", align_bytes=64) for u in range(2)]
+        m_half = H_HALF // PACK
 
         def deal(u, c):
             nc.scalar.copy(
-                w_pair[u][:, :, c * MH : (c + 1) * MH, :].rearrange("p e m j -> p m j e"),
+                w_pair[u][:, :, c * m_half : (c + 1) * m_half, :].rearrange("p e m j -> p m j e"),
                 w_half[c][:].rearrange("p j (m t) -> p m j t", t=PACK)[:, :, :, 2 * u : 2 * u + 2],
             )
 
@@ -108,8 +123,8 @@ def tile_picked_lapl_silu_e_kernel(
         x_scales = keep.tile([P, S], U8, align_bytes=64)
         for s in range(2):
             nc.vector.quantize_mx(
-                x_codes[:, s * SH : (s + 1) * SH].bitcast(FP8X4),
-                x_scales[:, s * SH : (s + 1) * SH],
+                x_codes[:, s * S_HALF : (s + 1) * S_HALF].bitcast(FP8X4),
+                x_scales[:, s * S_HALF : (s + 1) * S_HALF],
                 x_grouped[s][:].rearrange("p n j -> p (n j)"),
             )
 
@@ -140,53 +155,55 @@ def tile_picked_lapl_silu_e_kernel(
         deal(1, 0)
         deal(1, 1)
         quantise_w(0)
-        project(0, 0, SH)
-        project(0, SH, S)
+        project(0, 0, S_HALF)
+        project(0, S_HALF, S)
         for t in range(1, PACK):
             quantise_w(t)
             project(t, 0, S)
 
         less_first = keep.tile([P, PACK, V], F32)
         second = keep.tile([P, PACK, V], F32)
-
-        def neighbours(t):
+        for t in range(PACK):
             first = keep.tile([P, V], F32, name=f"first{t}")
             nc.vector.tensor_tensor(first[:], h[t][:].indirect(pos1_sb[:]), gate_sb[:, 0, :], MULT)
             nc.vector.tensor_tensor(second[:, t, :], h[t][:].indirect(pos2_sb[:]), gate_sb[:, 1, :], MULT)
-            nc.vector.tensor_tensor(less_first[:, t, :], h[t][:].indirect(cen_sb[:]), first[:], SUB)
+            width = V_HALF if t == PACK - 1 else V
+            for lo in range(0, V, width):
+                places = cen_sb[:, lo // STRIPE : (lo + width) // STRIPE]
+                nc.vector.tensor_tensor(
+                    less_first[:, t, lo : lo + width], h[t][:].indirect(places), first[:, lo : lo + width], SUB
+                )
 
-        for t in range(PACK):
-            neighbours(t)
-
-        z_grouped = [keep.tile([P, VH, PACK], BF16, name=f"z_grouped{b}", align_bytes=64) for b in range(2)]
-        z_codes = [keep.tile([P, VH], U32, name=f"z_codes{b}", align_bytes=64) for b in range(2)]
-        z_scales = [keep.tile([P, VH], U8, name=f"z_scales{b}", align_bytes=64) for b in range(2)]
+        z_grouped = [keep.tile([P, V_HALF, PACK], BF16, name=f"z_grouped{b}", align_bytes=64) for b in range(2)]
+        z_codes = [keep.tile([P, V_HALF], U32, name=f"z_codes{b}", align_bytes=64) for b in range(2)]
+        z_scales = [keep.tile([P, V_HALF], U8, name=f"z_scales{b}", align_bytes=64) for b in range(2)]
         for b in range(2):
-            vs = slice(b * VH, (b + 1) * VH)
+            targets = slice(b * V_HALF, (b + 1) * V_HALF)
             nc.vector.tensor_tensor(
                 z_grouped[b][:].rearrange("p (c i) t -> p c t i", i=2),
-                less_first[:, :, vs].rearrange("p t (c i) -> p c t i", i=2),
-                second[:, :, vs].rearrange("p t (c i) -> p c t i", i=2),
+                less_first[:, :, targets].rearrange("p t (c i) -> p c t i", i=2),
+                second[:, :, targets].rearrange("p t (c i) -> p c t i", i=2),
                 SUB,
             )
         for b in range(2):
             nc.vector.quantize_mx(
                 z_codes[b][:].bitcast(FP8X4), z_scales[b][:], z_grouped[b][:].rearrange("p v t -> p (v t)")
             )
+
         out_rows = out.rearrange("(g p) v -> p g v", p=P)
         for b in range(2):
-            result = keep.tile([P, 2, VH], F32, name=f"result{b}")
+            result = keep.tile([P, N // P, V_HALF], F32, name=f"result{b}")
             for g, copy in enumerate((nc.scalar.copy, nc.vector.tensor_copy)):
                 acc = bank(f"acc{b}_{g}")
-                ms = slice(g * P, (g + 1) * P)
+                rows = slice(g * P, (g + 1) * P)
                 nc.tensor.matmul_mx(
-                    acc[:, :VH],
-                    lhsT=w2_codes[:, ms].bitcast(FP8X4),
-                    lhsT_scale=w2_plane[:, ms],
+                    acc[:, :V_HALF],
+                    lhsT=w2_codes[:, rows].bitcast(FP8X4),
+                    lhsT_scale=w2_scale_sb[:, rows],
                     rhs=z_codes[b][:].bitcast(FP8X4),
                     rhs_scale=z_scales[b][:],
                     start=True,
                     stop=True,
                 )
-                copy(result[:, g, :], acc[:, :VH])
-            nc.sync.dma_start(out_rows[:, :, b * VH : (b + 1) * VH], result[:])
+                copy(result[:, g, :], acc[:, :V_HALF])
+            nc.sync.dma_start(out_rows[:, :, b * V_HALF : (b + 1) * V_HALF], result[:])

@@ -27,6 +27,8 @@ H_HALF = H // 2
 
 LOAD_NODES = (512, 256)
 SCALAR_NODES = 192
+SCALAR_LAST = 96
+P_HALF = P // 2
 RUN = 4
 
 
@@ -61,18 +63,18 @@ def tile_picked_lapl_silu_e_kernel(
         for c in range(2):
             nc.sync.dma_start(w_half[c][:], w_rows[:, :, c * H_HALF : (c + 1) * H_HALF])
         gate_sb = keep.tile([P, D, V], F32)
-        nc.sync.dma_start(gate_sb[:], gate.rearrange("d p v -> p d v"))
         pos1_sb = keep.tile([P, V // STRIPE], U16)
         pos2_sb = keep.tile([P, V // STRIPE], U16)
         cen_sb = keep.tile([P, V // STRIPE], U16)
         nc.sync.dma_start(pos1_sb[:], pos1)
+        nc.sync.dma_start(gate_sb[:], gate.rearrange("d p v -> p d v"))
         nc.sync.dma_start(pos2_sb[:], pos2)
         nc.sync.dma_start(cen_sb[:], cen)
 
         w2_codes = keep.tile([P, N], I32, align_bytes=64)
         nc.sync.dma_start(w2_codes[:], w2_words[0].rearrange("p n t -> p (n t)").bitcast(I32))
         w2_scale_sb = keep.tile([P, N], U8, align_bytes=64)
-        nc.gpsimd.memset(w2_scale_sb[:], 0)
+        nc.vector.memset(w2_scale_sb[:].bitcast(I32), 0)
         for q in range(P // QUADRANT):
             nc.sync.dma_start(
                 w2_scale_sb[QUADRANT * q : QUADRANT * q + 4, :].bitcast(I32),
@@ -103,21 +105,39 @@ def tile_picked_lapl_silu_e_kernel(
         pair_up(nc.scalar.copy, 0, first_nodes, 0, SCALAR_NODES)
         pair_up(nc.vector.tensor_copy, 0, first_nodes, SCALAR_NODES, first_nodes)
         gather_pairs(0)
-        for lo in range(0, T, second_nodes):
+        for lo in range(0, T - second_nodes, second_nodes):
             pair_up(nc.scalar.copy, 1, lo, 0, second_nodes)
+        pair_up(nc.scalar.copy, 1, T - second_nodes, 0, SCALAR_LAST)
+        pair_up(nc.vector.tensor_copy, 1, T - second_nodes, SCALAR_LAST, second_nodes)
         gather_pairs(1)
 
-        w_pair = [keep.tile([P, 2, P, PACK], BF16, name=f"w_pair{u}", align_bytes=64) for u in range(2)]
         m_half = H_HALF // PACK
+        w_early = [keep.tile([P, 2, m_half, PACK], BF16, name=f"w_early{c}", align_bytes=64) for c in range(2)]
+        w_late = keep.tile([P, 2, P, PACK], BF16, align_bytes=64)
 
-        def deal(u, c):
-            nc.scalar.copy(
-                w_pair[u][:, :, c * m_half : (c + 1) * m_half, :].rearrange("p e m j -> p m j e"),
+        def deal(copy, u, c):
+            dealt = w_early[c][:] if u == 0 else w_late[:, :, c * m_half : (c + 1) * m_half, :]
+            copy(
+                dealt.rearrange("p e m j -> p m j e"),
                 w_half[c][:].rearrange("p j (m t) -> p m j t", t=PACK)[:, :, :, 2 * u : 2 * u + 2],
             )
 
-        deal(0, 0)
-        deal(0, 1)
+        w_codes = [keep.tile([P, P], U32, name=f"w_codes{c}", align_bytes=64) for c in range(2)]
+        w_scales = [keep.tile([P, P], U8, name=f"w_scales{c}", align_bytes=64) for c in range(2)]
+        late_codes = keep.tile([P, 2 * P], U32, align_bytes=64)
+        late_scales = keep.tile([P, 2 * P], U8, align_bytes=64)
+        lhs = [(w_codes[c][:], w_scales[c][:]) for c in range(2)]
+        lhs.extend((late_codes[:, e * P : (e + 1) * P], late_scales[:, e * P : (e + 1) * P]) for e in range(2))
+        h = [keep.tile([P, S], F32, name=f"h{t}") for t in range(PACK)]
+
+        def quantise_early(c):
+            nc.vector.quantize_mx(
+                w_codes[c][:].bitcast(FP8X4), w_scales[c][:], w_early[c][:].rearrange("p e m j -> p (e m j)")
+            )
+
+        deal(nc.scalar.copy, 0, 0)
+        deal(nc.scalar.copy, 1, 0)
+        quantise_early(0)
 
         x_codes = keep.tile([P, S], U32, align_bytes=64)
         x_scales = keep.tile([P, S], U8, align_bytes=64)
@@ -128,23 +148,13 @@ def tile_picked_lapl_silu_e_kernel(
                 x_grouped[s][:].rearrange("p n j -> p (n j)"),
             )
 
-        w_codes = [keep.tile([P, P], U32, name=f"w_codes{t}", align_bytes=64) for t in range(PACK)]
-        w_scales = [keep.tile([P, P], U8, name=f"w_scales{t}", align_bytes=64) for t in range(PACK)]
-        h = [keep.tile([P, S], F32, name=f"h{t}") for t in range(PACK)]
-
-        def quantise_w(t):
-            nc.vector.quantize_mx(
-                w_codes[t][:].bitcast(FP8X4),
-                w_scales[t][:],
-                w_pair[t // 2][:, t % 2, :, :].rearrange("p m j -> p (m j)"),
-            )
-
         def project(t, lo, hi):
             acc = bank(f"pre{t}_{lo}")
+            codes, scales = lhs[t]
             nc.tensor.matmul_mx(
                 acc[:, : hi - lo],
-                lhsT=w_codes[t][:].bitcast(FP8X4),
-                lhsT_scale=w_scales[t][:],
+                lhsT=codes.bitcast(FP8X4),
+                lhsT_scale=scales,
                 rhs=x_codes[:, lo:hi].bitcast(FP8X4),
                 rhs_scale=x_scales[:, lo:hi],
                 start=True,
@@ -152,27 +162,37 @@ def tile_picked_lapl_silu_e_kernel(
             )
             nc.scalar.activation(h[t][:, lo:hi], acc[:, : hi - lo], SILU)
 
-        deal(1, 0)
-        deal(1, 1)
-        quantise_w(0)
         project(0, 0, S_HALF)
         project(0, S_HALF, S)
+        deal(nc.vector.tensor_copy, 0, 1)
+        deal(nc.vector.tensor_copy, 1, 1)
+        quantise_early(1)
+        nc.vector.quantize_mx(
+            late_codes[:].bitcast(FP8X4), late_scales[:], w_late[:].rearrange("p e m j -> p (e m j)")
+        )
         for t in range(1, PACK):
-            quantise_w(t)
             project(t, 0, S)
 
-        less_first = keep.tile([P, PACK, V], F32)
-        second = keep.tile([P, PACK, V], F32)
+        terms = keep.tile([P, PACK, 2, V], F32)
         for t in range(PACK):
+            early = keep.tile([P, 2, V], F32, name=f"early{t}") if t < 2 else None
+            made = early[:] if t < 2 else terms[:, t, :, :]
             first = keep.tile([P, V], F32, name=f"first{t}")
             nc.vector.tensor_tensor(first[:], h[t][:].indirect(pos1_sb[:]), gate_sb[:, 0, :], MULT)
-            nc.vector.tensor_tensor(second[:, t, :], h[t][:].indirect(pos2_sb[:]), gate_sb[:, 1, :], MULT)
+            nc.vector.tensor_tensor(made[:, 1, :], h[t][:].indirect(pos2_sb[:]), gate_sb[:, 1, :], MULT)
             width = V_HALF if t == PACK - 1 else V
             for lo in range(0, V, width):
                 places = cen_sb[:, lo // STRIPE : (lo + width) // STRIPE]
                 nc.vector.tensor_tensor(
-                    less_first[:, t, lo : lo + width], h[t][:].indirect(places), first[:, lo : lo + width], SUB
+                    made[:, 0, lo : lo + width], h[t][:].indirect(places), first[:, lo : lo + width], SUB
                 )
+            if t < 2:
+                for e in range(2):
+                    nc.sync.dma_start(
+                        terms[t * P_HALF : (t + 1) * P_HALF, e, :, :], early[e * P_HALF : (e + 1) * P_HALF, :, :]
+                    )
+        less_first = terms[:, :, 0, :]
+        second = terms[:, :, 1, :]
 
         z_grouped = [keep.tile([P, V_HALF, PACK], BF16, name=f"z_grouped{b}", align_bytes=64) for b in range(2)]
         z_codes = [keep.tile([P, V_HALF], U32, name=f"z_codes{b}", align_bytes=64) for b in range(2)]

@@ -1,6 +1,7 @@
 from contextlib import ExitStack
 
 import concourse.mybir as mybir
+from concourse.masks import make_identity
 
 K, T, S, D, V, H, N = 512, 1024, 512, 2, 256, 512, 256
 FLOPS = 2 * K * H * S + 2 * H * N * V
@@ -14,6 +15,7 @@ U8 = mybir.dt.uint8
 FP8X4 = mybir.dt.float8_e4m3fn_x4
 MULT = mybir.AluOpType.mult
 SUB = mybir.AluOpType.subtract
+ADD = mybir.AluOpType.add
 SILU = mybir.ActivationFunctionType.Silu
 
 P = 128
@@ -39,15 +41,20 @@ def tile_picked_lapl_silu_e_kernel(
 
     with ExitStack() as ctx:
         keep = ctx.enter_context(tc.tile_pool(name="keep", bufs=1))
-        psum = ctx.enter_context(tc.psum_pool(name="psum", bufs=8))
+        psum = ctx.enter_context(tc.psum_pool(name="psum", bufs=7))
 
-        def bank(name):
+        def bank(name, last=False):
+            if last:
+                return psum.tile([P, BANK], F32, name=name, tag="last", bufs=1)
             return psum.tile([P, BANK], F32, name=name, tag="bank")
 
         warm = keep.tile([P, 8], F32)
         nc.vector.memset(warm[:], 0.0)
         warm_out = keep.tile([P, 8], F32)
         nc.scalar.activation(warm_out[:], warm[:], SILU)
+
+        identity = keep.tile([P, P], F32)
+        make_identity(nc, identity[:])
 
         x_rows = xT.rearrange("(p j) t -> p j t", j=PACK)
         w_rows = w1.rearrange("(p j) c -> p j c", j=PACK)
@@ -63,11 +70,11 @@ def tile_picked_lapl_silu_e_kernel(
         for c in range(2):
             nc.sync.dma_start(w_half[c][:], w_rows[:, :, c * H_HALF : (c + 1) * H_HALF])
         gate_sb = keep.tile([P, D, V], F32)
+        nc.sync.dma_start(gate_sb[:], gate.rearrange("d p v -> p d v"))
         pos1_sb = keep.tile([P, V // STRIPE], U16)
         pos2_sb = keep.tile([P, V // STRIPE], U16)
         cen_sb = keep.tile([P, V // STRIPE], U16)
         nc.sync.dma_start(pos1_sb[:], pos1)
-        nc.sync.dma_start(gate_sb[:], gate.rearrange("d p v -> p d v"))
         nc.sync.dma_start(pos2_sb[:], pos2)
         nc.sync.dma_start(cen_sb[:], cen)
 
@@ -149,7 +156,7 @@ def tile_picked_lapl_silu_e_kernel(
             )
 
         def project(t, lo, hi):
-            acc = bank(f"pre{t}_{lo}")
+            acc = bank(f"pre{t}_{lo}", last=t == PACK - 1)
             codes, scales = lhs[t]
             nc.tensor.matmul_mx(
                 acc[:, : hi - lo],
@@ -162,6 +169,8 @@ def tile_picked_lapl_silu_e_kernel(
             )
             nc.scalar.activation(h[t][:, lo:hi], acc[:, : hi - lo], SILU)
 
+        minus_gate = keep.tile([P, V], F32)
+        nc.scalar.mul(minus_gate[:], gate_sb[:, 1, :], -1.0)
         project(0, 0, S_HALF)
         project(0, S_HALF, S)
         deal(nc.vector.tensor_copy, 0, 1)
@@ -173,41 +182,63 @@ def tile_picked_lapl_silu_e_kernel(
         for t in range(1, PACK):
             project(t, 0, S)
 
-        terms = keep.tile([P, PACK, 2, V], F32)
-        for t in range(PACK):
-            early = keep.tile([P, 2, V], F32, name=f"early{t}") if t < 2 else None
-            made = early[:] if t < 2 else terms[:, t, :, :]
+        z_flat = keep.tile([P, V * PACK], BF16, align_bytes=64)
+        z_grouped = z_flat[:].rearrange("p (v t) -> p v t", t=PACK)
+        z_words = z_flat[:].bitcast(F32).rearrange("p (v u) -> p v u", u=2)
+        z_codes = [keep.tile([P, V_HALF], U32, name=f"z_codes{b}", align_bytes=64) for b in range(2)]
+        z_scales = [keep.tile([P, V_HALF], U8, name=f"z_scales{b}", align_bytes=64) for b in range(2)]
+        turned = bank("turned", last=True)
+        back = bank("back")
+        for t in range(2):
+            made = keep.tile([P, 3, V], F32, name=f"made{t}")
+            nc.vector.tensor_tensor(made[:, 0, :], h[t][:].indirect(pos1_sb[:]), gate_sb[:, 0, :], MULT)
+            nc.vector.tensor_tensor(made[:, 1, :], h[t][:].indirect(pos2_sb[:]), minus_gate[:], MULT)
+            nc.vector.tensor_tensor(made[:, 2, :], h[t][:].indirect(cen_sb[:]), made[:, 0, :], SUB)
+            for b in range(2):
+                lo = (2 * b + t) * P
+                for term in (1, 2):
+                    nc.tensor.matmul(
+                        turned[:, lo : lo + P],
+                        lhsT=made[:, term, b * V_HALF : (b + 1) * V_HALF],
+                        rhs=identity[:],
+                        is_transpose=True,
+                        start=term == 1,
+                        stop=term == 2,
+                    )
+        z_pairs = keep.tile([P, 2, P, 2], BF16)
+        nc.scalar.copy(
+            z_pairs[:].rearrange("v b (c m) e -> v (b c) m e", c=2),
+            turned[:].rearrange("v (bc e m) -> v bc m e", bc=4, e=2),
+        )
+        for b in range(2):
+            nc.tensor.transpose(
+                back[:, b * P : (b + 1) * P], z_pairs[:, b, :, :].rearrange("v p e -> v (p e)").bitcast(F32), identity[:]
+            )
+        nc.scalar.copy(z_words[:, :, 0], back[:, :V])
+
+        terms = keep.tile([P, 2, 2, V], F32)
+        for e in range(2):
+            t = 2 + e
             first = keep.tile([P, V], F32, name=f"first{t}")
             nc.vector.tensor_tensor(first[:], h[t][:].indirect(pos1_sb[:]), gate_sb[:, 0, :], MULT)
-            nc.vector.tensor_tensor(made[:, 1, :], h[t][:].indirect(pos2_sb[:]), gate_sb[:, 1, :], MULT)
+            nc.vector.tensor_tensor(terms[:, e, 1, :], h[t][:].indirect(pos2_sb[:]), minus_gate[:], MULT)
             width = V_HALF if t == PACK - 1 else V
             for lo in range(0, V, width):
                 places = cen_sb[:, lo // STRIPE : (lo + width) // STRIPE]
                 nc.vector.tensor_tensor(
-                    made[:, 0, lo : lo + width], h[t][:].indirect(places), first[:, lo : lo + width], SUB
+                    terms[:, e, 0, lo : lo + width], h[t][:].indirect(places), first[:, lo : lo + width], SUB
                 )
-            if t < 2:
-                for e in range(2):
-                    nc.sync.dma_start(
-                        terms[t * P_HALF : (t + 1) * P_HALF, e, :, :], early[e * P_HALF : (e + 1) * P_HALF, :, :]
-                    )
-        less_first = terms[:, :, 0, :]
-        second = terms[:, :, 1, :]
-
-        z_grouped = [keep.tile([P, V_HALF, PACK], BF16, name=f"z_grouped{b}", align_bytes=64) for b in range(2)]
-        z_codes = [keep.tile([P, V_HALF], U32, name=f"z_codes{b}", align_bytes=64) for b in range(2)]
-        z_scales = [keep.tile([P, V_HALF], U8, name=f"z_scales{b}", align_bytes=64) for b in range(2)]
         for b in range(2):
             targets = slice(b * V_HALF, (b + 1) * V_HALF)
             nc.vector.tensor_tensor(
-                z_grouped[b][:].rearrange("p (c i) t -> p c t i", i=2),
-                less_first[:, :, targets].rearrange("p t (c i) -> p c t i", i=2),
-                second[:, :, targets].rearrange("p t (c i) -> p c t i", i=2),
-                SUB,
+                z_grouped[:, targets, 2:].rearrange("p (c i) e -> p c e i", i=2),
+                terms[:, :, 0, targets].rearrange("p e (c i) -> p c e i", i=2),
+                terms[:, :, 1, targets].rearrange("p e (c i) -> p c e i", i=2),
+                ADD,
             )
         for b in range(2):
             nc.vector.quantize_mx(
-                z_codes[b][:].bitcast(FP8X4), z_scales[b][:], z_grouped[b][:].rearrange("p v t -> p (v t)")
+                z_codes[b][:].bitcast(FP8X4), z_scales[b][:], z_flat[:, b * V_HALF * PACK : (b + 1) * V_HALF * PACK]
             )
 
         out_rows = out.rearrange("(g p) v -> p g v", p=P)

@@ -15,7 +15,6 @@ U8 = mybir.dt.uint8
 FP8X4 = mybir.dt.float8_e4m3fn_x4
 MULT = mybir.AluOpType.mult
 SUB = mybir.AluOpType.subtract
-ADD = mybir.AluOpType.add
 SILU = mybir.ActivationFunctionType.Silu
 
 P = 128
@@ -53,6 +52,8 @@ def tile_picked_lapl_silu_e_kernel(
         warm_out = keep.tile([P, 8], F32)
         nc.scalar.activation(warm_out[:], warm[:], SILU)
 
+        minus_one = keep.tile([P, V], F32)
+        nc.vector.memset(minus_one[:], -1.0)
         identity = keep.tile([P, P], F32)
         make_identity(nc, identity[:])
 
@@ -169,8 +170,6 @@ def tile_picked_lapl_silu_e_kernel(
             )
             nc.scalar.activation(h[t][:, lo:hi], acc[:, : hi - lo], SILU)
 
-        minus_gate = keep.tile([P, V], F32)
-        nc.scalar.mul(minus_gate[:], gate_sb[:, 1, :], -1.0)
         project(0, 0, S_HALF)
         project(0, S_HALF, S)
         deal(nc.vector.tensor_copy, 0, 1)
@@ -192,23 +191,24 @@ def tile_picked_lapl_silu_e_kernel(
         for t in range(2):
             made = keep.tile([P, 3, V], F32, name=f"made{t}")
             nc.vector.tensor_tensor(made[:, 0, :], h[t][:].indirect(pos1_sb[:]), gate_sb[:, 0, :], MULT)
-            nc.vector.tensor_tensor(made[:, 1, :], h[t][:].indirect(pos2_sb[:]), minus_gate[:], MULT)
-            nc.vector.tensor_tensor(made[:, 2, :], h[t][:].indirect(cen_sb[:]), made[:, 0, :], SUB)
+            nc.vector.tensor_tensor(made[:, 1, :], h[t][:].indirect(pos2_sb[:]), gate_sb[:, 1, :], MULT)
+            nc.vector.tensor_tensor(made[:, 2, :], h[t][:].indirect(cen_sb[:]), minus_one[:], MULT)
             for b in range(2):
                 lo = (2 * b + t) * P
-                for term in (1, 2):
+                for term in range(3):
                     nc.tensor.matmul(
                         turned[:, lo : lo + P],
                         lhsT=made[:, term, b * V_HALF : (b + 1) * V_HALF],
                         rhs=identity[:],
                         is_transpose=True,
-                        start=term == 1,
+                        start=term == 0,
                         stop=term == 2,
                     )
         z_pairs = keep.tile([P, 2, P, 2], BF16)
-        nc.scalar.copy(
+        nc.scalar.mul(
             z_pairs[:].rearrange("v b (c m) e -> v (b c) m e", c=2),
             turned[:].rearrange("v (bc e m) -> v bc m e", bc=4, e=2),
+            -1.0,
         )
         for b in range(2):
             nc.tensor.transpose(
@@ -221,7 +221,7 @@ def tile_picked_lapl_silu_e_kernel(
             t = 2 + e
             first = keep.tile([P, V], F32, name=f"first{t}")
             nc.vector.tensor_tensor(first[:], h[t][:].indirect(pos1_sb[:]), gate_sb[:, 0, :], MULT)
-            nc.vector.tensor_tensor(terms[:, e, 1, :], h[t][:].indirect(pos2_sb[:]), minus_gate[:], MULT)
+            nc.vector.tensor_tensor(terms[:, e, 1, :], h[t][:].indirect(pos2_sb[:]), gate_sb[:, 1, :], MULT)
             width = V_HALF if t == PACK - 1 else V
             for lo in range(0, V, width):
                 places = cen_sb[:, lo // STRIPE : (lo + width) // STRIPE]
@@ -234,7 +234,7 @@ def tile_picked_lapl_silu_e_kernel(
                 z_grouped[:, targets, 2:].rearrange("p (c i) e -> p c e i", i=2),
                 terms[:, :, 0, targets].rearrange("p e (c i) -> p c e i", i=2),
                 terms[:, :, 1, targets].rearrange("p e (c i) -> p c e i", i=2),
-                ADD,
+                SUB,
             )
         for b in range(2):
             nc.vector.quantize_mx(

@@ -29,8 +29,9 @@ H_HALF = H // 2
 LOAD_NODES = (512, 256)
 SCALAR_NODES = 192
 SCALAR_LAST = 96
-P_HALF = P // 2
 RUN = 4
+RING_BANKS = 7
+WARM_COLUMNS = 8
 
 
 def tile_picked_lapl_silu_e_kernel(
@@ -40,16 +41,16 @@ def tile_picked_lapl_silu_e_kernel(
 
     with ExitStack() as ctx:
         keep = ctx.enter_context(tc.tile_pool(name="keep", bufs=1))
-        psum = ctx.enter_context(tc.psum_pool(name="psum", bufs=7))
+        psum = ctx.enter_context(tc.psum_pool(name="psum", bufs=RING_BANKS))
 
-        def bank(name, last=False):
-            if last:
+        def bank(name, shared=False):
+            if shared:
                 return psum.tile([P, BANK], F32, name=name, tag="last", bufs=1)
             return psum.tile([P, BANK], F32, name=name, tag="bank")
 
-        warm = keep.tile([P, 8], F32)
+        warm = keep.tile([P, WARM_COLUMNS], F32)
         nc.vector.memset(warm[:], 0.0)
-        warm_out = keep.tile([P, 8], F32)
+        warm_out = keep.tile([P, WARM_COLUMNS], F32)
         nc.scalar.activation(warm_out[:], warm[:], SILU)
 
         minus_one = keep.tile([P, V], F32)
@@ -157,7 +158,7 @@ def tile_picked_lapl_silu_e_kernel(
             )
 
         def project(t, lo, hi):
-            acc = bank(f"pre{t}_{lo}", last=t == PACK - 1)
+            acc = bank(f"pre{t}_{lo}", shared=t == PACK - 1)
             codes, scales = lhs[t]
             nc.tensor.matmul_mx(
                 acc[:, : hi - lo],
@@ -186,7 +187,7 @@ def tile_picked_lapl_silu_e_kernel(
         z_words = z_flat[:].bitcast(F32).rearrange("p (v u) -> p v u", u=2)
         z_codes = [keep.tile([P, V_HALF], U32, name=f"z_codes{b}", align_bytes=64) for b in range(2)]
         z_scales = [keep.tile([P, V_HALF], U8, name=f"z_scales{b}", align_bytes=64) for b in range(2)]
-        turned = bank("turned", last=True)
+        turned = bank("turned", shared=True)
         back = bank("back")
         for t in range(2):
             made = keep.tile([P, 3, V], F32, name=f"made{t}")
@@ -217,18 +218,15 @@ def tile_picked_lapl_silu_e_kernel(
         nc.scalar.copy(z_words[:, :, 0], back[:, :V])
 
         terms = keep.tile([P, 2, 2, V], F32)
-        for e in range(2):
-            t = 2 + e
-            first = keep.tile([P, V], F32, name=f"first{t}")
-            nc.vector.tensor_tensor(first[:], h[t][:].indirect(pos1_sb[:]), gate_sb[:, 0, :], MULT)
-            nc.vector.tensor_tensor(terms[:, e, 1, :], h[t][:].indirect(pos2_sb[:]), gate_sb[:, 1, :], MULT)
-            width = V_HALF if t == PACK - 1 else V
-            for lo in range(0, V, width):
-                places = cen_sb[:, lo // STRIPE : (lo + width) // STRIPE]
-                nc.vector.tensor_tensor(
-                    terms[:, e, 0, lo : lo + width], h[t][:].indirect(places), first[:, lo : lo + width], SUB
-                )
-        for b in range(2):
+        first = [keep.tile([P, V], F32, name=f"first{e}") for e in range(2)]
+
+        def gather_terms(e, lo, hi):
+            window = h[2 + e][:]
+            cols = slice(lo // STRIPE, hi // STRIPE)
+            nc.vector.tensor_tensor(terms[:, e, 1, lo:hi], window.indirect(pos2_sb[:, cols]), gate_sb[:, 1, lo:hi], MULT)
+            nc.vector.tensor_tensor(terms[:, e, 0, lo:hi], window.indirect(cen_sb[:, cols]), first[e][:, lo:hi], SUB)
+
+        def finish(b):
             targets = slice(b * V_HALF, (b + 1) * V_HALF)
             nc.vector.tensor_tensor(
                 z_grouped[:, targets, 2:].rearrange("p (c i) e -> p c e i", i=2),
@@ -236,25 +234,39 @@ def tile_picked_lapl_silu_e_kernel(
                 terms[:, :, 1, targets].rearrange("p e (c i) -> p c e i", i=2),
                 SUB,
             )
-        for b in range(2):
             nc.vector.quantize_mx(
                 z_codes[b][:].bitcast(FP8X4), z_scales[b][:], z_flat[:, b * V_HALF * PACK : (b + 1) * V_HALF * PACK]
             )
 
-        out_rows = out.rearrange("(g p) v -> p g v", p=P)
+        nc.vector.tensor_tensor(first[0][:], h[2][:].indirect(pos1_sb[:]), gate_sb[:, 0, :], MULT)
+        gather_terms(0, 0, V)
+        nc.vector.tensor_tensor(first[1][:], h[3][:].indirect(pos1_sb[:]), gate_sb[:, 0, :], MULT)
         for b in range(2):
-            result = keep.tile([P, N // P, V_HALF], F32, name=f"result{b}")
-            for g, copy in enumerate((nc.scalar.copy, nc.vector.tensor_copy)):
-                acc = bank(f"acc{b}_{g}")
-                rows = slice(g * P, (g + 1) * P)
-                nc.tensor.matmul_mx(
-                    acc[:, :V_HALF],
-                    lhsT=w2_codes[:, rows].bitcast(FP8X4),
-                    lhsT_scale=w2_scale_sb[:, rows],
-                    rhs=z_codes[b][:].bitcast(FP8X4),
-                    rhs_scale=z_scales[b][:],
-                    start=True,
-                    stop=True,
-                )
-                copy(result[:, g, :], acc[:, :V_HALF])
-            nc.sync.dma_start(out_rows[:, :, b * V_HALF : (b + 1) * V_HALF], result[:])
+            gather_terms(1, b * V_HALF, (b + 1) * V_HALF)
+            finish(b)
+
+        out_rows = out.rearrange("(g p) v -> p g v", p=P)
+
+        def multiply(b, g, copy, result):
+            acc = bank(f"acc{b}_{g}")
+            rows = slice(g * P, (g + 1) * P)
+            nc.tensor.matmul_mx(
+                acc[:, :V_HALF],
+                lhsT=w2_codes[:, rows].bitcast(FP8X4),
+                lhsT_scale=w2_scale_sb[:, rows],
+                rhs=z_codes[b][:].bitcast(FP8X4),
+                rhs_scale=z_scales[b][:],
+                start=True,
+                stop=True,
+            )
+            copy(result[:, g, :], acc[:, :V_HALF])
+
+        result0 = keep.tile([P, N // P, V_HALF], F32)
+        for g in range(N // P):
+            multiply(0, g, nc.scalar.copy, result0)
+        nc.sync.dma_start(out_rows[:, :, :V_HALF], result0[:])
+
+        result1 = keep.tile([P, N // P, V_HALF], F32)
+        for g, copy in enumerate((nc.scalar.copy, nc.vector.tensor_copy)):
+            multiply(1, g, copy, result1)
+            nc.sync.dma_start(out_rows[:, g, V_HALF:], result1[:, g, :])

@@ -16,6 +16,7 @@ FP8X4 = mybir.dt.float8_e4m3fn_x4
 MULT = mybir.AluOpType.mult
 SUB = mybir.AluOpType.subtract
 SILU = mybir.ActivationFunctionType.Silu
+COPY = mybir.ActivationFunctionType.Copy
 
 P = 128
 PACK = 4
@@ -53,8 +54,6 @@ def tile_picked_lapl_silu_e_kernel(
         warm_out = keep.tile([P, WARM_COLUMNS], F32)
         nc.scalar.activation(warm_out[:], warm[:], SILU)
 
-        minus_one = keep.tile([P, V], F32)
-        nc.vector.memset(minus_one[:], -1.0)
         identity = keep.tile([P, P], F32)
         make_identity(nc, identity[:])
 
@@ -190,16 +189,17 @@ def tile_picked_lapl_silu_e_kernel(
         turned = bank("turned", shared=True)
         back = bank("back")
         for t in range(2):
-            made = keep.tile([P, 3, V], F32, name=f"made{t}")
+            made = keep.tile([P, 2, V], F32, name=f"made{t}")
             nc.vector.tensor_tensor(made[:, 0, :], h[t][:].indirect(pos1_sb[:]), gate_sb[:, 0, :], MULT)
             nc.vector.tensor_tensor(made[:, 1, :], h[t][:].indirect(pos2_sb[:]), gate_sb[:, 1, :], MULT)
-            nc.vector.tensor_tensor(made[:, 2, :], h[t][:].indirect(cen_sb[:]), minus_one[:], MULT)
+            centre = keep.tile([P, V], F32, name=f"centre{t}")
+            nc.scalar.activation(centre[:], h[t][:].indirect(cen_sb[:]), COPY, scale=-1.0)
             for b in range(2):
                 lo = (2 * b + t) * P
                 for term in range(3):
                     nc.tensor.matmul(
                         turned[:, lo : lo + P],
-                        lhsT=made[:, term, b * V_HALF : (b + 1) * V_HALF],
+                        lhsT=(made[:, term, :] if term < 2 else centre[:])[:, b * V_HALF : (b + 1) * V_HALF],
                         rhs=identity[:],
                         is_transpose=True,
                         start=term == 0,
@@ -218,13 +218,14 @@ def tile_picked_lapl_silu_e_kernel(
         nc.scalar.copy(z_words[:, :, 0], back[:, :V])
 
         terms = keep.tile([P, 2, 2, V], F32)
-        first = [keep.tile([P, V], F32, name=f"first{e}") for e in range(2)]
+        first = keep.tile([P, 2, V], F32)
+        centres = keep.tile([P, 2, V], F32)
+        for e in range(2):
+            nc.scalar.activation(centres[:, e, :], h[2 + e][:].indirect(cen_sb[:]), COPY)
 
-        def gather_terms(e, lo, hi):
-            window = h[2 + e][:]
+        def gather_second(e, lo, hi):
             cols = slice(lo // STRIPE, hi // STRIPE)
-            nc.vector.tensor_tensor(terms[:, e, 1, lo:hi], window.indirect(pos2_sb[:, cols]), gate_sb[:, 1, lo:hi], MULT)
-            nc.vector.tensor_tensor(terms[:, e, 0, lo:hi], window.indirect(cen_sb[:, cols]), first[e][:, lo:hi], SUB)
+            nc.vector.tensor_tensor(terms[:, e, 1, lo:hi], h[2 + e][:].indirect(pos2_sb[:, cols]), gate_sb[:, 1, lo:hi], MULT)
 
         def finish(b):
             targets = slice(b * V_HALF, (b + 1) * V_HALF)
@@ -238,11 +239,13 @@ def tile_picked_lapl_silu_e_kernel(
                 z_codes[b][:].bitcast(FP8X4), z_scales[b][:], z_flat[:, b * V_HALF * PACK : (b + 1) * V_HALF * PACK]
             )
 
-        nc.vector.tensor_tensor(first[0][:], h[2][:].indirect(pos1_sb[:]), gate_sb[:, 0, :], MULT)
-        gather_terms(0, 0, V)
-        nc.vector.tensor_tensor(first[1][:], h[3][:].indirect(pos1_sb[:]), gate_sb[:, 0, :], MULT)
+        nc.vector.tensor_tensor(first[:, 0, :], h[2][:].indirect(pos1_sb[:]), gate_sb[:, 0, :], MULT)
+        gather_second(0, 0, V)
+        nc.vector.tensor_tensor(first[:, 1, :], h[3][:].indirect(pos1_sb[:]), gate_sb[:, 0, :], MULT)
+        gather_second(1, 0, V_HALF)
+        nc.vector.tensor_tensor(terms[:, :, 0, :], centres[:], first[:], SUB)
+        gather_second(1, V_HALF, V)
         for b in range(2):
-            gather_terms(1, b * V_HALF, (b + 1) * V_HALF)
             finish(b)
 
         out_rows = out.rearrange("(g p) v -> p g v", p=P)

@@ -27,10 +27,6 @@ S_HALF = S // 2
 V_HALF = V // 2
 H_HALF = H // 2
 
-LOAD_NODES = (512, 256)
-SCALAR_NODES = 192
-SCALAR_LAST = 96
-RUN = 4
 RING_BANKS = 7
 WARM_COLUMNS = 8
 
@@ -59,14 +55,12 @@ def tile_picked_lapl_silu_e_kernel(
 
         x_rows = xT.rearrange("(p j) t -> p j t", j=PACK)
         w_rows = w1.rearrange("(p j) c -> p j c", j=PACK)
-        x_load = {}
+        planes = [keep.tile([P, T], F32, name=f"plane{j}") for j in range(PACK)]
         offs_sb = keep.tile([P, S // STRIPE], U16)
-        for u, nodes in enumerate(LOAD_NODES):
-            for lo in range(0, T, nodes):
-                x_load[u, lo] = keep.tile([P, 2, nodes], F32, name=f"x_load{u}_{lo}")
-                nc.sync.dma_start(x_load[u, lo][:], x_rows[:, 2 * u : 2 * u + 2, lo : lo + nodes])
-                if (u, lo) == (0, 0):
-                    nc.sync.dma_start(offs_sb[:], offs)
+        for j in range(PACK):
+            nc.sync.dma_start(planes[j][:], x_rows[:, j, :])
+            if j == 0:
+                nc.sync.dma_start(offs_sb[:], offs)
         w_half = [keep.tile([P, PACK, H_HALF], F32, name=f"w_half{c}") for c in range(2)]
         for c in range(2):
             nc.sync.dma_start(w_half[c][:], w_rows[:, :, c * H_HALF : (c + 1) * H_HALF])
@@ -89,35 +83,22 @@ def tile_picked_lapl_silu_e_kernel(
                 w2_scales[0, 4 * q : 4 * q + 4, :].bitcast(I32),
             )
 
-        pairs = [keep.tile([P, T, 2], BF16, name=f"pairs{u}") for u in range(2)]
         x_grouped = [keep.tile([P, S_HALF, PACK], BF16, name=f"x_grouped{s}", align_bytes=64) for s in range(2)]
+        picked = [keep.tile([P, 2, S_HALF], BF16, name=f"picked{u}") for u in range(2)]
         offs_cols = S_HALF // STRIPE
 
-        def pair_up(copy, u, lo, first_node, end_node):
+        def weave(copy, u):
             copy(
-                pairs[u][:, lo + first_node : lo + end_node, :].rearrange("p (c i) e -> p c e i", i=RUN),
-                x_load[u, lo][:, :, first_node:end_node].rearrange("p e (c i) -> p c e i", i=RUN),
+                x_grouped[1][:, :, 2 * u : 2 * u + 2].rearrange("p (c i) e -> p c e i", i=2),
+                picked[u][:].rearrange("p e (c i) -> p c e i", i=2),
             )
 
-        def gather_pairs(u):
-            window = pairs[u][:].rearrange("p n e -> p (n e)").bitcast(U32)
-            for s in range(2):
-                grouped = x_grouped[s][:].rearrange("p n j -> p (n j)").bitcast(U32)
-                nc.vector.tensor_copy(
-                    grouped.rearrange("p (n u) -> p n u", u=2)[:, :, u],
-                    window.indirect(offs_sb[:, s * offs_cols : (s + 1) * offs_cols]),
-                )
-
-        first_nodes, second_nodes = LOAD_NODES
-        pair_up(nc.scalar.copy, 0, 0, 0, first_nodes)
-        pair_up(nc.scalar.copy, 0, first_nodes, 0, SCALAR_NODES)
-        pair_up(nc.vector.tensor_copy, 0, first_nodes, SCALAR_NODES, first_nodes)
-        gather_pairs(0)
-        for lo in range(0, T - second_nodes, second_nodes):
-            pair_up(nc.scalar.copy, 1, lo, 0, second_nodes)
-        pair_up(nc.scalar.copy, 1, T - second_nodes, 0, SCALAR_LAST)
-        pair_up(nc.vector.tensor_copy, 1, T - second_nodes, SCALAR_LAST, second_nodes)
-        gather_pairs(1)
+        for j in range(PACK):
+            nc.vector.tensor_copy(x_grouped[0][:, :, j], planes[j][:].indirect(offs_sb[:, :offs_cols]))
+            nc.scalar.activation(picked[j // 2][:, j % 2, :], planes[j][:].indirect(offs_sb[:, offs_cols:]), COPY)
+            if j == 1:
+                weave(nc.scalar.copy, 0)
+        weave(nc.vector.tensor_copy, 1)
 
         m_half = H_HALF // PACK
         w_early = [keep.tile([P, 2, m_half, PACK], BF16, name=f"w_early{c}", align_bytes=64) for c in range(2)]

@@ -55,7 +55,7 @@ def tile_picked_lapl_silu_e_kernel(
 
         x_rows = xT.rearrange("(p j) t -> p j t", j=PACK)
         w_rows = w1.rearrange("(p j) c -> p j c", j=PACK)
-        planes = [keep.tile([P, T], F32, name=f"plane{j}") for j in range(PACK)]
+        planes = [keep.tile([P, T], F32, name=f"plane{j}", tag=f"plane{j}", align_bytes=64) for j in range(PACK)]
         offs_sb = keep.tile([P, S // STRIPE], U16)
         for j in range(PACK):
             nc.sync.dma_start(planes[j][:], x_rows[:, j, :])
@@ -65,13 +65,13 @@ def tile_picked_lapl_silu_e_kernel(
         for c in range(2):
             nc.sync.dma_start(w_half[c][:], w_rows[:, :, c * H_HALF : (c + 1) * H_HALF])
         gate_sb = keep.tile([P, D, V], F32)
-        nc.sync.dma_start(gate_sb[:], gate.rearrange("d p v -> p d v"))
         pos1_sb = keep.tile([P, V // STRIPE], U16)
         pos2_sb = keep.tile([P, V // STRIPE], U16)
         cen_sb = keep.tile([P, V // STRIPE], U16)
+        nc.sync.dma_start(cen_sb[:], cen)
         nc.sync.dma_start(pos1_sb[:], pos1)
         nc.sync.dma_start(pos2_sb[:], pos2)
-        nc.sync.dma_start(cen_sb[:], cen)
+        nc.sync.dma_start(gate_sb[:], gate.rearrange("d p v -> p d v"))
 
         w2_codes = keep.tile([P, N], I32, align_bytes=64)
         nc.sync.dma_start(w2_codes[:], w2_words[0].rearrange("p n t -> p (n t)").bitcast(I32))
@@ -104,11 +104,11 @@ def tile_picked_lapl_silu_e_kernel(
         w_early = [keep.tile([P, 2, m_half, PACK], BF16, name=f"w_early{c}", align_bytes=64) for c in range(2)]
         w_late = keep.tile([P, 2, P, PACK], BF16, align_bytes=64)
 
-        def deal(copy, u, c):
+        def deal(copy, u, c, columns=slice(0, m_half)):
             dealt = w_early[c][:] if u == 0 else w_late[:, :, c * m_half : (c + 1) * m_half, :]
             copy(
-                dealt.rearrange("p e m j -> p m j e"),
-                w_half[c][:].rearrange("p j (m t) -> p m j t", t=PACK)[:, :, :, 2 * u : 2 * u + 2],
+                dealt.rearrange("p e m j -> p m j e")[:, columns],
+                w_half[c][:].rearrange("p j (m t) -> p m j t", t=PACK)[:, columns, :, 2 * u : 2 * u + 2],
             )
 
         w_codes = [keep.tile([P, P], U32, name=f"w_codes{c}", align_bytes=64) for c in range(2)]
@@ -128,7 +128,7 @@ def tile_picked_lapl_silu_e_kernel(
         deal(nc.scalar.copy, 1, 0)
         quantise_early(0)
 
-        x_codes = keep.tile([P, S], U32, align_bytes=64)
+        x_codes = keep.tile([P, S], U32, tag=f"plane{PACK - 1}", align_bytes=64)
         x_scales = keep.tile([P, S], U8, align_bytes=64)
         for s in range(2):
             nc.vector.quantize_mx(
@@ -138,7 +138,7 @@ def tile_picked_lapl_silu_e_kernel(
             )
 
         def project(t, lo, hi):
-            acc = bank(f"pre{t}_{lo}", shared=t == PACK - 1)
+            acc = bank(f"pre{t}_{lo}", shared=(t, lo) == (1, S_HALF))
             codes, scales = lhs[t]
             nc.tensor.matmul_mx(
                 acc[:, : hi - lo],
@@ -151,15 +151,20 @@ def tile_picked_lapl_silu_e_kernel(
             )
             nc.scalar.activation(h[t][:, lo:hi], acc[:, : hi - lo], SILU)
 
+        deal(nc.scalar.copy, 1, 1, slice(m_half // 4, m_half))
         project(0, 0, S_HALF)
         project(0, S_HALF, S)
         deal(nc.vector.tensor_copy, 0, 1)
-        deal(nc.vector.tensor_copy, 1, 1)
+        deal(nc.vector.tensor_copy, 1, 1, slice(0, m_half // 4))
         quantise_early(1)
         nc.vector.quantize_mx(
             late_codes[:].bitcast(FP8X4), late_scales[:], w_late[:].rearrange("p e m j -> p (e m j)")
         )
-        for t in range(1, PACK):
+        project(1, 0, S_HALF)
+        project(1, S_HALF, S)
+        centre = [keep.tile([P, V], F32, name=f"centre{t}") for t in range(2)]
+        nc.scalar.activation(centre[0][:], h[0][:].indirect(cen_sb[:]), COPY, scale=-1.0)
+        for t in range(2, PACK):
             project(t, 0, S)
 
         z_flat = keep.tile([P, V * PACK], BF16, align_bytes=64)
@@ -168,66 +173,58 @@ def tile_picked_lapl_silu_e_kernel(
         z_codes = [keep.tile([P, V_HALF], U32, name=f"z_codes{b}", align_bytes=64) for b in range(2)]
         z_scales = [keep.tile([P, V_HALF], U8, name=f"z_scales{b}", align_bytes=64) for b in range(2)]
         turned = bank("turned", shared=True)
-        back = bank("back")
+        made = [keep.tile([P, V], F32, name=f"made{n}") for n in range(4)]
         for t in range(2):
-            made = keep.tile([P, 2, V], F32, name=f"made{t}")
-            nc.vector.tensor_tensor(made[:, 0, :], h[t][:].indirect(pos1_sb[:]), gate_sb[:, 0, :], MULT)
-            nc.vector.tensor_tensor(made[:, 1, :], h[t][:].indirect(pos2_sb[:]), gate_sb[:, 1, :], MULT)
-            centre = keep.tile([P, V], F32, name=f"centre{t}")
-            nc.scalar.activation(centre[:], h[t][:].indirect(cen_sb[:]), COPY, scale=-1.0)
+            nc.vector.tensor_tensor(made[2 * t][:], h[t][:].indirect(pos1_sb[:]), gate_sb[:, 0, :], MULT)
+            nc.vector.tensor_tensor(made[2 * t + 1][:], h[t][:].indirect(pos2_sb[:]), gate_sb[:, 1, :], MULT)
+        nc.scalar.activation(centre[1][:], h[1][:].indirect(cen_sb[:]), COPY, scale=-1.0)
+        arrivals = [(made[0], 0), (centre[0], 0), (made[1], 0), (made[2], 1), (made[3], 1), (centre[1], 1)]
+        for n, (term, t) in enumerate(arrivals):
             for b in range(2):
                 lo = (2 * b + t) * P
-                for term in range(3):
-                    nc.tensor.matmul(
-                        turned[:, lo : lo + P],
-                        lhsT=(made[:, term, :] if term < 2 else centre[:])[:, b * V_HALF : (b + 1) * V_HALF],
-                        rhs=identity[:],
-                        is_transpose=True,
-                        start=term == 0,
-                        stop=term == 2,
-                    )
-        z_pairs = keep.tile([P, 2, P, 2], BF16)
-        nc.scalar.mul(
-            z_pairs[:].rearrange("v b (c m) e -> v (b c) m e", c=2),
-            turned[:].rearrange("v (bc e m) -> v bc m e", bc=4, e=2),
-            -1.0,
-        )
+                nc.tensor.matmul(
+                    turned[:, lo : lo + P],
+                    lhsT=term[:, b * V_HALF : (b + 1) * V_HALF],
+                    rhs=identity[:],
+                    is_transpose=True,
+                    start=(n, b) == (0, 0),
+                    stop=(n, b) == (len(arrivals) - 1, 1),
+                )
+        z_pairs = [keep.tile([P, P, 2], BF16, name=f"z_pairs{b}") for b in range(2)]
+        back = [bank(f"back{b}") for b in range(2)]
         for b in range(2):
-            nc.tensor.transpose(
-                back[:, b * P : (b + 1) * P], z_pairs[:, b, :, :].rearrange("v p e -> v (p e)").bitcast(F32), identity[:]
+            nc.scalar.mul(
+                z_pairs[b][:].rearrange("v (c m) e -> v c m e", c=2),
+                turned[:, 2 * b * P : 2 * (b + 1) * P].rearrange("v (c e m) -> v c m e", c=2, e=2),
+                -1.0,
             )
-        nc.scalar.copy(z_words[:, :, 0], back[:, :V])
+            nc.tensor.transpose(back[b][:, :P], z_pairs[b][:].rearrange("v p e -> v (p e)").bitcast(F32), identity[:])
+        for b in range(2):
+            nc.scalar.copy(z_words[:, b * V_HALF : (b + 1) * V_HALF, 0], back[b][:, :P])
 
-        terms = keep.tile([P, 2, 2, V], F32)
-        first = keep.tile([P, 2, V], F32)
         centres = keep.tile([P, 2, V], F32)
+        partial = keep.tile([P, 2, V], F32)
         for e in range(2):
             nc.scalar.activation(centres[:, e, :], h[2 + e][:].indirect(cen_sb[:]), COPY)
-
-        def gather_second(e, lo, hi):
-            cols = slice(lo // STRIPE, hi // STRIPE)
-            nc.vector.tensor_tensor(terms[:, e, 1, lo:hi], h[2 + e][:].indirect(pos2_sb[:, cols]), gate_sb[:, 1, lo:hi], MULT)
-
-        def finish(b):
+        terms = keep.tile([P, 4, V], F32)
+        for e in range(2):
+            nc.vector.tensor_tensor(terms[:, 2 + e, :], h[2 + e][:].indirect(pos1_sb[:]), gate_sb[:, 0, :], MULT)
+            nc.vector.tensor_tensor(terms[:, e, :], h[2 + e][:].indirect(pos2_sb[:]), gate_sb[:, 1, :], MULT)
+        for b in range(2):
+            targets = slice(b * V_HALF, (b + 1) * V_HALF)
+            nc.vector.tensor_tensor(partial[:, :, targets], centres[:, :, targets], terms[:, 2:, targets], SUB)
+        for b in range(2):
             targets = slice(b * V_HALF, (b + 1) * V_HALF)
             nc.vector.tensor_tensor(
                 z_grouped[:, targets, 2:].rearrange("p (c i) e -> p c e i", i=2),
-                terms[:, :, 0, targets].rearrange("p e (c i) -> p c e i", i=2),
-                terms[:, :, 1, targets].rearrange("p e (c i) -> p c e i", i=2),
+                partial[:, :, targets].rearrange("p e (c i) -> p c e i", i=2),
+                terms[:, :2, targets].rearrange("p e (c i) -> p c e i", i=2),
                 SUB,
             )
+        for b in range(2):
             nc.vector.quantize_mx(
                 z_codes[b][:].bitcast(FP8X4), z_scales[b][:], z_flat[:, b * V_HALF * PACK : (b + 1) * V_HALF * PACK]
             )
-
-        nc.vector.tensor_tensor(first[:, 0, :], h[2][:].indirect(pos1_sb[:]), gate_sb[:, 0, :], MULT)
-        gather_second(0, 0, V)
-        nc.vector.tensor_tensor(first[:, 1, :], h[3][:].indirect(pos1_sb[:]), gate_sb[:, 0, :], MULT)
-        gather_second(1, 0, V_HALF)
-        nc.vector.tensor_tensor(terms[:, :, 0, :], centres[:], first[:], SUB)
-        gather_second(1, V_HALF, V)
-        for b in range(2):
-            finish(b)
 
         out_rows = out.rearrange("(g p) v -> p g v", p=P)
 

@@ -87,17 +87,18 @@ def tile_picked_lapl_silu_e_kernel(
         picked = [keep.tile([P, 2, S_HALF], BF16, name=f"picked{u}") for u in range(2)]
         offs_cols = S_HALF // STRIPE
 
-        def weave(copy, u):
+        def weave(copy, u, nodes=slice(0, S_HALF)):
             copy(
-                x_grouped[1][:, :, 2 * u : 2 * u + 2].rearrange("p (c i) e -> p c e i", i=2),
-                picked[u][:].rearrange("p e (c i) -> p c e i", i=2),
+                x_grouped[1][:, nodes, 2 * u : 2 * u + 2].rearrange("p (c i) e -> p c e i", i=2),
+                picked[u][:, :, nodes].rearrange("p e (c i) -> p c e i", i=2),
             )
 
         for j in range(PACK):
             nc.vector.tensor_copy(x_grouped[0][:, :, j], planes[j][:].indirect(offs_sb[:, :offs_cols]))
             nc.scalar.activation(picked[j // 2][:, j % 2, :], planes[j][:].indirect(offs_sb[:, offs_cols:]), COPY)
             if j == 1:
-                weave(nc.scalar.copy, 0)
+                weave(nc.scalar.copy, 0, slice(0, S_HALF // 2))
+                weave(nc.vector.tensor_copy, 0, slice(S_HALF // 2, S_HALF))
         weave(nc.vector.tensor_copy, 1)
 
         m_half = H_HALF // PACK

@@ -118,7 +118,7 @@ def tile_picked_lapl_silu_e_kernel(
         late_scales = keep.tile([P, 2 * P], U8, align_bytes=64)
         lhs = [(w_codes[c][:], w_scales[c][:]) for c in range(2)]
         lhs.extend((late_codes[:, e * P : (e + 1) * P], late_scales[:, e * P : (e + 1) * P]) for e in range(2))
-        h = [keep.tile([P, S], F32, name=f"h{t}") for t in range(PACK)]
+        h = [keep.tile([P, S], F32, name=f"h{t}", tag=f"h{t}", align_bytes=64) for t in range(PACK)]
 
         def quantise_early(c):
             nc.vector.quantize_mx(
@@ -163,16 +163,11 @@ def tile_picked_lapl_silu_e_kernel(
         )
         project(1, 0, S_HALF)
         project(1, S_HALF, S)
-        centre = [keep.tile([P, V], F32, name=f"centre{t}") for t in range(2)]
+        centre = [keep.tile([P, V], F32, name=f"centre{t}", tag=f"centre{t}") for t in range(2)]
         nc.scalar.activation(centre[0][:], h[0][:].indirect(cen_sb[:]), COPY, scale=-1.0)
         for t in range(2, PACK):
             project(t, 0, S)
 
-        z_flat = keep.tile([P, V * PACK], BF16, align_bytes=64)
-        z_grouped = z_flat[:].rearrange("p (v t) -> p v t", t=PACK)
-        z_words = z_flat[:].bitcast(F32).rearrange("p (v u) -> p v u", u=2)
-        z_codes = [keep.tile([P, V_HALF], U32, name=f"z_codes{b}", align_bytes=64) for b in range(2)]
-        z_scales = [keep.tile([P, V_HALF], U8, name=f"z_scales{b}", align_bytes=64) for b in range(2)]
         turned = bank("turned", shared=True)
         made = [keep.tile([P, V], F32, name=f"made{n}") for n in range(4)]
         for t in range(2):
@@ -200,20 +195,33 @@ def tile_picked_lapl_silu_e_kernel(
                 -1.0,
             )
             nc.tensor.transpose(back[b][:, :P], z_pairs[b][:].rearrange("v p e -> v (p e)").bitcast(F32), identity[:])
-        for b in range(2):
-            nc.scalar.copy(z_words[:, b * V_HALF : (b + 1) * V_HALF, 0], back[b][:, :P])
 
         centres = keep.tile([P, 2, V], F32)
         partial = keep.tile([P, 2, V], F32)
         for e in range(2):
             nc.scalar.activation(centres[:, e, :], h[2 + e][:].indirect(cen_sb[:]), COPY)
         terms = keep.tile([P, 4, V], F32)
-        for e in range(2):
-            nc.vector.tensor_tensor(terms[:, 2 + e, :], h[2 + e][:].indirect(pos1_sb[:]), gate_sb[:, 0, :], MULT)
-            nc.vector.tensor_tensor(terms[:, e, :], h[2 + e][:].indirect(pos2_sb[:]), gate_sb[:, 1, :], MULT)
+        half_list = V_HALF // STRIPE
+        nc.vector.tensor_tensor(terms[:, 2, :], h[2][:].indirect(pos1_sb[:]), gate_sb[:, 0, :], MULT)
+        nc.vector.tensor_tensor(terms[:, 0, :], h[2][:].indirect(pos2_sb[:]), gate_sb[:, 1, :], MULT)
+        nc.vector.tensor_tensor(terms[:, 3, :], h[3][:].indirect(pos1_sb[:]), gate_sb[:, 0, :], MULT)
+        nc.vector.tensor_tensor(
+            terms[:, 1, :V_HALF], h[3][:].indirect(pos2_sb[:, :half_list]), gate_sb[:, 1, :V_HALF], MULT
+        )
+        fetched = keep.tile([P, V_HALF], F32, tag="centre1")
+        nc.scalar.activation(fetched[:], h[3][:].indirect(pos2_sb[:, half_list:]), COPY)
         for b in range(2):
             targets = slice(b * V_HALF, (b + 1) * V_HALF)
             nc.vector.tensor_tensor(partial[:, :, targets], centres[:, :, targets], terms[:, 2:, targets], SUB)
+        nc.vector.tensor_tensor(terms[:, 1, V_HALF:], fetched[:], gate_sb[:, 1, V_HALF:], MULT)
+
+        z_flat = keep.tile([P, V * PACK], BF16, tag=f"h{PACK - 1}", align_bytes=64)
+        z_grouped = z_flat[:].rearrange("p (v t) -> p v t", t=PACK)
+        z_words = z_flat[:].bitcast(F32).rearrange("p (v u) -> p v u", u=2)
+        z_codes = [keep.tile([P, V_HALF], U32, name=f"z_codes{b}", align_bytes=64) for b in range(2)]
+        z_scales = [keep.tile([P, V_HALF], U8, name=f"z_scales{b}", align_bytes=64) for b in range(2)]
+        for b in range(2):
+            nc.scalar.copy(z_words[:, b * V_HALF : (b + 1) * V_HALF, 0], back[b][:, :P])
         for b in range(2):
             targets = slice(b * V_HALF, (b + 1) * V_HALF)
             nc.vector.tensor_tensor(

@@ -152,18 +152,17 @@ def tile_picked_lapl_silu_e_kernel(
             )
             nc.scalar.activation(h[t][:, lo:hi], acc[:, : hi - lo], SILU)
 
-        deal(nc.scalar.copy, 1, 1, slice(m_half // 4, m_half))
-        project(0, 0, S_HALF)
-        project(0, S_HALF, S)
+        for lo in range(0, S, P):
+            project(0, lo, lo + P)
         deal(nc.vector.tensor_copy, 0, 1)
-        deal(nc.vector.tensor_copy, 1, 1, slice(0, m_half // 4))
+        deal(nc.vector.tensor_copy, 1, 1)
         quantise_early(1)
         nc.vector.quantize_mx(
             late_codes[:].bitcast(FP8X4), late_scales[:], w_late[:].rearrange("p e m j -> p (e m j)")
         )
         project(1, 0, S_HALF)
         project(1, S_HALF, S)
-        centre = [keep.tile([P, V], F32, name=f"centre{t}", tag=f"centre{t}") for t in range(2)]
+        centre = [keep.tile([P, V], F32, name=f"centre{t}", tag=tag, align_bytes=64) for t, tag in enumerate(("w_codes1", "centre1"))]
         nc.scalar.activation(centre[0][:], h[0][:].indirect(cen_sb[:]), COPY, scale=-1.0)
         for t in range(2, PACK):
             project(t, 0, S)
@@ -208,7 +207,7 @@ def tile_picked_lapl_silu_e_kernel(
         nc.vector.tensor_tensor(
             terms[:, 1, :V_HALF], h[3][:].indirect(pos2_sb[:, :half_list]), gate_sb[:, 1, :V_HALF], MULT
         )
-        fetched = keep.tile([P, V_HALF], F32, tag="centre1")
+        fetched = keep.tile([P, V_HALF], F32, tag="centre1", align_bytes=64)
         nc.scalar.activation(fetched[:], h[3][:].indirect(pos2_sb[:, half_list:]), COPY)
         for b in range(2):
             targets = slice(b * V_HALF, (b + 1) * V_HALF)
@@ -252,8 +251,8 @@ def tile_picked_lapl_silu_e_kernel(
             copy(result[:, g, :], acc[:, :V_HALF])
 
         result0 = keep.tile([P, N // P, V_HALF], F32)
-        for g in range(N // P):
-            multiply(0, g, nc.scalar.copy, result0)
+        for g, copy in enumerate((nc.scalar.copy, nc.vector.tensor_copy)):
+            multiply(0, g, copy, result0)
         nc.sync.dma_start(out_rows[:, :, :V_HALF], result0[:])
 
         result1 = keep.tile([P, N // P, V_HALF], F32)

from contextlib import ExitStack

import concourse.mybir as mybir
from concourse.masks import make_identity

K, T, S, D, V, H, N = 512, 1024, 512, 2, 256, 512, 256
FLOPS = 2 * K * H * S + 2 * H * N * V

F32 = mybir.dt.float32
BF16 = mybir.dt.bfloat16
I32 = mybir.dt.int32
U32 = mybir.dt.uint32
U16 = mybir.dt.uint16
U8 = mybir.dt.uint8
FP8X4 = mybir.dt.float8_e4m3fn_x4
MULT = mybir.AluOpType.mult
SUB = mybir.AluOpType.subtract
SILU = mybir.ActivationFunctionType.Silu
COPY = mybir.ActivationFunctionType.Copy

P = 128
PACK = 4
STRIPE = 16
BANK = 512
QUADRANT = 32
S_HALF = S // 2
V_HALF = V // 2
H_HALF = H // 2

RING_BANKS = 7
WARM_COLUMNS = 8


def tile_picked_lapl_silu_e_kernel(
    tc, xT, w1, w2_words, w2_scales, gate, offs, cen, pos1, pos2, out
):
    nc = tc.nc

    with ExitStack() as ctx:
        keep = ctx.enter_context(tc.tile_pool(name="keep", bufs=1))
        psum = ctx.enter_context(tc.psum_pool(name="psum", bufs=RING_BANKS))

        def bank(name, shared=False):
            if shared:
                return psum.tile([P, BANK], F32, name=name, tag="last", bufs=1)
            return psum.tile([P, BANK], F32, name=name, tag="bank")

        warm = keep.tile([P, WARM_COLUMNS], F32)
        nc.vector.memset(warm[:], 0.0)
        warm_out = keep.tile([P, WARM_COLUMNS], F32)
        nc.scalar.activation(warm_out[:], warm[:], SILU)

        identity = keep.tile([P, P], F32)
        make_identity(nc, identity[:])

        x_rows = xT.rearrange("(p j) t -> p j t", j=PACK)
        w_rows = w1.rearrange("(p j) c -> p j c", j=PACK)
        planes = [keep.tile([P, T], F32, name=f"plane{j}", tag=f"plane{j}", align_bytes=64) for j in range(PACK)]
        offs_sb = keep.tile([P, S // STRIPE], U16)
        for j in range(PACK):
            nc.sync.dma_start(planes[j][:], x_rows[:, j, :])
            if j == 0:
                nc.sync.dma_start(offs_sb[:], offs)
        w_half = [keep.tile([P, PACK, H_HALF], F32, name=f"w_half{c}") for c in range(2)]
        for c in range(2):
            nc.sync.dma_start(w_half[c][:], w_rows[:, :, c * H_HALF : (c + 1) * H_HALF])
        gate_sb = keep.tile([P, D, V], F32)
        pos1_sb = keep.tile([P, V // STRIPE], U16)
        pos2_sb = keep.tile([P, V // STRIPE], U16)
        cen_sb = keep.tile([P, V // STRIPE], U16)
        nc.sync.dma_start(cen_sb[:], cen)
        nc.sync.dma_start(pos1_sb[:], pos1)
        nc.sync.dma_start(pos2_sb[:], pos2)
        nc.sync.dma_start(gate_sb[:], gate.rearrange("d p v -> p d v"))

        w2_codes = keep.tile([P, N], I32, align_bytes=64)
        nc.sync.dma_start(w2_codes[:], w2_words[0].rearrange("p n t -> p (n t)").bitcast(I32))
        w2_scale_sb = keep.tile([P, N], U8, align_bytes=64)
        nc.vector.memset(w2_scale_sb[:].bitcast(I32), 0)
        for q in range(P // QUADRANT):
            nc.sync.dma_start(
                w2_scale_sb[QUADRANT * q : QUADRANT * q + 4, :].bitcast(I32),
                w2_scales[0, 4 * q : 4 * q + 4, :].bitcast(I32),
            )

        x_grouped = [keep.tile([P, S_HALF, PACK], BF16, name=f"x_grouped{s}", align_bytes=64) for s in range(2)]
        picked = [keep.tile([P, 2, S_HALF], BF16, name=f"picked{u}") for u in range(2)]
        offs_cols = S_HALF // STRIPE

        def weave(copy, u, nodes=slice(0, S_HALF)):
            copy(
                x_grouped[1][:, nodes, 2 * u : 2 * u + 2].rearrange("p (c i) e -> p c e i", i=2),
                picked[u][:, :, nodes].rearrange("p e (c i) -> p c e i", i=2),
            )

        for j in range(PACK):
            nc.vector.tensor_copy(x_grouped[0][:, :, j], planes[j][:].indirect(offs_sb[:, :offs_cols]))
            nc.scalar.activation(picked[j // 2][:, j % 2, :], planes[j][:].indirect(offs_sb[:, offs_cols:]), COPY)
            if j == 1:
                weave(nc.scalar.copy, 0, slice(0, S_HALF // 2))
                weave(nc.vector.tensor_copy, 0, slice(S_HALF // 2, S_HALF))
        weave(nc.vector.tensor_copy, 1)

        m_half = H_HALF // PACK
        w_early = [keep.tile([P, 2, m_half, PACK], BF16, name=f"w_early{c}", align_bytes=64) for c in range(2)]
        w_late = keep.tile([P, 2, P, PACK], BF16, align_bytes=64)

        def deal(copy, u, c, columns=slice(0, m_half)):
            dealt = w_early[c][:] if u == 0 else w_late[:, :, c * m_half : (c + 1) * m_half, :]
            copy(
                dealt.rearrange("p e m j -> p m j e")[:, columns],
                w_half[c][:].rearrange("p j (m t) -> p m j t", t=PACK)[:, columns, :, 2 * u : 2 * u + 2],
            )

        w_codes = [keep.tile([P, P], U32, name=f"w_codes{c}", align_bytes=64) for c in range(2)]
        w_scales = [keep.tile([P, P], U8, name=f"w_scales{c}", align_bytes=64) for c in range(2)]
        late_codes = keep.tile([P, 2 * P], U32, align_bytes=64)
        late_scales = keep.tile([P, 2 * P], U8, align_bytes=64)
        lhs = [(w_codes[c][:], w_scales[c][:]) for c in range(2)]
        lhs.extend((late_codes[:, e * P : (e + 1) * P], late_scales[:, e * P : (e + 1) * P]) for e in range(2))
        h = [keep.tile([P, S], F32, name=f"h{t}", tag=f"h{t}", align_bytes=64) for t in range(PACK)]

        def quantise_early(c):
            nc.vector.quantize_mx(
                w_codes[c][:].bitcast(FP8X4), w_scales[c][:], w_early[c][:].rearrange("p e m j -> p (e m j)")
            )

        deal(nc.scalar.copy, 0, 0)
        deal(nc.scalar.copy, 1, 0)
        quantise_early(0)

        x_codes = keep.tile([P, S], U32, tag=f"plane{PACK - 1}", align_bytes=64)
        x_scales = keep.tile([P, S], U8, align_bytes=64)
        for s in range(2):
            nc.vector.quantize_mx(
                x_codes[:, s * S_HALF : (s + 1) * S_HALF].bitcast(FP8X4),
                x_scales[:, s * S_HALF : (s + 1) * S_HALF],
                x_grouped[s][:].rearrange("p n j -> p (n j)"),
            )

        def project(t, lo, hi):
            acc = bank(f"pre{t}_{lo}", shared=(t, lo) == (1, S_HALF))
            codes, scales = lhs[t]
            nc.tensor.matmul_mx(
                acc[:, : hi - lo],
                lhsT=codes.bitcast(FP8X4),
                lhsT_scale=scales,
                rhs=x_codes[:, lo:hi].bitcast(FP8X4),
                rhs_scale=x_scales[:, lo:hi],
                start=True,
                stop=True,
            )
            nc.scalar.activation(h[t][:, lo:hi], acc[:, : hi - lo], SILU)

        for lo in range(0, S, P):
            project(0, lo, lo + P)
        deal(nc.vector.tensor_copy, 0, 1)
        deal(nc.vector.tensor_copy, 1, 1)
        quantise_early(1)
        nc.vector.quantize_mx(
            late_codes[:].bitcast(FP8X4), late_scales[:], w_late[:].rearrange("p e m j -> p (e m j)")
        )
        project(1, 0, S_HALF)
        project(1, S_HALF, S)
        centre = [keep.tile([P, V], F32, name=f"centre{t}", tag=tag, align_bytes=64) for t, tag in enumerate(("w_codes1", "centre1"))]
        nc.scalar.activation(centre[0][:], h[0][:].indirect(cen_sb[:]), COPY, scale=-1.0)
        for t in range(2, PACK):
            project(t, 0, S)

        turned = bank("turned", shared=True)
        made = [keep.tile([P, V], F32, name=f"made{n}") for n in range(4)]
        for t in range(2):
            nc.vector.tensor_tensor(made[2 * t][:], h[t][:].indirect(pos1_sb[:]), gate_sb[:, 0, :], MULT)
            nc.vector.tensor_tensor(made[2 * t + 1][:], h[t][:].indirect(pos2_sb[:]), gate_sb[:, 1, :], MULT)
        nc.scalar.activation(centre[1][:], h[1][:].indirect(cen_sb[:]), COPY, scale=-1.0)
        arrivals = [(made[0], 0), (centre[0], 0), (made[1], 0), (made[2], 1), (made[3], 1), (centre[1], 1)]
        for n, (term, t) in enumerate(arrivals):
            for b in range(2):
                lo = (2 * b + t) * P
                nc.tensor.matmul(
                    turned[:, lo : lo + P],
                    lhsT=term[:, b * V_HALF : (b + 1) * V_HALF],
                    rhs=identity[:],
                    is_transpose=True,
                    start=(n, b) == (0, 0),
                    stop=(n, b) == (len(arrivals) - 1, 1),
                )
        z_pairs = [keep.tile([P, P, 2], BF16, name=f"z_pairs{b}") for b in range(2)]
        back = [bank(f"back{b}") for b in range(2)]
        for b in range(2):
            nc.scalar.mul(
                z_pairs[b][:].rearrange("v (c m) e -> v c m e", c=2),
                turned[:, 2 * b * P : 2 * (b + 1) * P].rearrange("v (c e m) -> v c m e", c=2, e=2),
                -1.0,
            )
            nc.tensor.transpose(back[b][:, :P], z_pairs[b][:].rearrange("v p e -> v (p e)").bitcast(F32), identity[:])

        centres = keep.tile([P, 2, V], F32)
        partial = keep.tile([P, 2, V], F32)
        for e in range(2):
            nc.scalar.activation(centres[:, e, :], h[2 + e][:].indirect(cen_sb[:]), COPY)
        terms = keep.tile([P, 4, V], F32)
        half_list = V_HALF // STRIPE
        nc.vector.tensor_tensor(terms[:, 2, :], h[2][:].indirect(pos1_sb[:]), gate_sb[:, 0, :], MULT)
        nc.vector.tensor_tensor(terms[:, 0, :], h[2][:].indirect(pos2_sb[:]), gate_sb[:, 1, :], MULT)
        nc.vector.tensor_tensor(terms[:, 3, :], h[3][:].indirect(pos1_sb[:]), gate_sb[:, 0, :], MULT)
        nc.vector.tensor_tensor(
            terms[:, 1, :V_HALF], h[3][:].indirect(pos2_sb[:, :half_list]), gate_sb[:, 1, :V_HALF], MULT
        )
        fetched = keep.tile([P, V_HALF], F32, tag="centre1", align_bytes=64)
        nc.scalar.activation(fetched[:], h[3][:].indirect(pos2_sb[:, half_list:]), COPY)
        for b in range(2):
            targets = slice(b * V_HALF, (b + 1) * V_HALF)
            nc.vector.tensor_tensor(partial[:, :, targets], centres[:, :, targets], terms[:, 2:, targets], SUB)
        nc.vector.tensor_tensor(terms[:, 1, V_HALF:], fetched[:], gate_sb[:, 1, V_HALF:], MULT)

        z_flat = keep.tile([P, V * PACK], BF16, tag=f"h{PACK - 1}", align_bytes=64)
        z_grouped = z_flat[:].rearrange("p (v t) -> p v t", t=PACK)
        z_words = z_flat[:].bitcast(F32).rearrange("p (v u) -> p v u", u=2)
        z_codes = [keep.tile([P, V_HALF], U32, name=f"z_codes{b}", align_bytes=64) for b in range(2)]
        z_scales = [keep.tile([P, V_HALF], U8, name=f"z_scales{b}", align_bytes=64) for b in range(2)]
        for b in range(2):
            nc.scalar.copy(z_words[:, b * V_HALF : (b + 1) * V_HALF, 0], back[b][:, :P])
        for b in range(2):
            targets = slice(b * V_HALF, (b + 1) * V_HALF)
            nc.vector.tensor_tensor(
                z_grouped[:, targets, 2:].rearrange("p (c i) e -> p c e i", i=2),
                partial[:, :, targets].rearrange("p e (c i) -> p c e i", i=2),
                terms[:, :2, targets].rearrange("p e (c i) -> p c e i", i=2),
                SUB,
            )
        for b in range(2):
            nc.vector.quantize_mx(
                z_codes[b][:].bitcast(FP8X4), z_scales[b][:], z_flat[:, b * V_HALF * PACK : (b + 1) * V_HALF * PACK]
            )

        out_rows = out.rearrange("(g p) v -> p g v", p=P)

        def multiply(b, g, copy, result):
            acc = bank(f"acc{b}_{g}")
            rows = slice(g * P, (g + 1) * P)
            nc.tensor.matmul_mx(
                acc[:, :V_HALF],
                lhsT=w2_codes[:, rows].bitcast(FP8X4),
                lhsT_scale=w2_scale_sb[:, rows],
                rhs=z_codes[b][:].bitcast(FP8X4),
                rhs_scale=z_scales[b][:],
                start=True,
                stop=True,
            )
            copy(result[:, g, :], acc[:, :V_HALF])

        result0 = keep.tile([P, N // P, V_HALF], F32)
        for g, copy in enumerate((nc.scalar.copy, nc.vector.tensor_copy)):
            multiply(0, g, copy, result0)
        nc.sync.dma_start(out_rows[:, :, :V_HALF], result0[:])

        result1 = keep.tile([P, N // P, V_HALF], F32)
        for g, copy in enumerate((nc.scalar.copy, nc.vector.tensor_copy)):
            multiply(1, g, copy, result1)
            nc.sync.dma_start(out_rows[:, g, V_HALF:], result1[:, g, :])
